import numpy as np
import ml_dtypes


def mxq(x, axis, fmt="e4m3"):
    dtype, down = {"e4m3": (ml_dtypes.float8_e4m3fn, 7), "e5m2": (ml_dtypes.float8_e5m2, 14)}[fmt]
    v = np.moveaxis(np.asarray(x, np.float32).astype(ml_dtypes.bfloat16).astype(np.float64), axis, -1)
    blocks = v.reshape(v.shape[:-1] + (-1, 32))
    amax = np.abs(blocks).max(-1, keepdims=True)
    byte = np.maximum(np.where(amax > 0, np.frexp(amax)[1] - 1 + 127, 0) - down, 1)
    scale = np.exp2(byte - 127.0)
    codes = (blocks / scale).astype(np.float32).astype(dtype).astype(np.float64)
    return np.moveaxis((codes * scale).reshape(v.shape), -1, axis)


WIDE = False


def mx_kscale(k):
    if not WIDE:
        return np.ones(k)
    levels = np.array([10, -10, 5, -5, 0])
    if k % 512:
        return np.exp2(np.random.permutation(np.resize(levels, k // 32))).repeat(32)
    a = np.empty((k // 512, 16))
    for p in range(k // 512):
        a[p, :8] = np.random.permutation(np.resize(levels, 8))
        for g in range(8):
            far = levels[np.abs(levels - a[p, g]) >= 10]
            a[p, g + 8] = far[np.random.randint(len(far))]
    return np.exp2(a.ravel()).repeat(32)


def f64(x):
    return np.asarray(x).astype(np.float64)


def striped(idx):
    return np.tile(idx.reshape(-1, 16).T, (8, 1)).astype(np.uint16)


def unstriped(offs):
    return offs[:16].T.reshape(-1).astype(np.int64)


E2M1 = np.array([0.0, 0.5, 1.0, 1.5, 2.0, 3.0, 4.0, 6.0, -0.0, -0.5, -1.0, -1.5, -2.0, -3.0, -4.0, -6.0])


def pack_weight(w, fmt):
    k, n = w.shape
    w = f64(np.asarray(w, np.float32).astype(ml_dtypes.bfloat16)).reshape(k // 32, 32, n)
    amax = np.abs(w).max(1)
    if fmt == "e4m3":
        byte = np.frexp(amax)[1] - 1 + 127 - 7
    else:
        mant, ex = np.frexp(amax / 6.0)
        byte = np.where(mant > 0.5, ex, ex - 1) + 127
    byte = np.clip(np.where(amax > 0, byte, 1), 1, 254)
    scaled = (w * np.exp2(127.0 - byte)[:, None, :]).reshape(k, n).astype(np.float32)
    by_word = np.ascontiguousarray(scaled.reshape(k // 512, 128, 4, n).transpose(0, 1, 3, 2))
    if fmt == "e4m3":
        words = by_word.astype(ml_dtypes.float8_e4m3fn).view(np.uint8)
    else:
        c = by_word.astype(ml_dtypes.float4_e2m1fn).view(np.uint8) & 0xF
        words = (c[..., 0::2] | (c[..., 1::2] << 4)).reshape(k // 512, 128, 2 * n)
    return np.ascontiguousarray(words), np.ascontiguousarray(byte.astype(np.uint8).reshape(k // 512, 16, n))


def unpack_weight(words, scales, fmt):
    g, _, n = scales.shape
    words = np.ascontiguousarray(words).reshape(g, 128, n, -1)
    if fmt == "e4m3":
        vals = words.view(ml_dtypes.float8_e4m3fn).astype(np.float64)
    else:
        nib = np.empty((g, 128, n, 4), np.uint8)
        nib[..., 0::2] = words & 0xF
        nib[..., 1::2] = words >> 4
        vals = E2M1[nib]
    vals = vals * np.repeat(np.exp2(scales.astype(np.float64) - 127.0), 8, axis=1)[..., None]
    return vals.transpose(0, 1, 3, 2).reshape(g * 512, n)


def gelu(v):
    return 0.5 * v * (1.0 + np.tanh(np.sqrt(2.0 / np.pi) * (v + 0.044715 * v**3)))


K, T, S, H, T3, S2, T2 = 1024, 2048, 512, 1024, 2048, 512, 1024

def setup_inputs():
    n = np.random.standard_normal
    s = mx_kscale(K)[:, None]
    u = s
    tab_words, tab_scales = pack_weight(n((K, T)) * s, "e4m3")
    tab2_words, tab2_scales = pack_weight(n((H, T3)) / np.sqrt(H) / u, "e4m3")
    w3_words, w3_scales = pack_weight(1.2 * n((K, H)) / np.sqrt(K) / s * u.T, "e2m1")
    return {
        "tab_words": tab_words, "tab_scales": tab_scales,
        "offs": striped(np.random.permutation(T)[:S]),
        "w1": (1.2 * n((K, H)) / np.sqrt(K) / s).astype(np.float32),
        "w2": (0.54 * n((K, H)) / np.sqrt(K) / s).astype(np.float32),
        "w3_words": w3_words, "w3_scales": w3_scales,
        "gain": (2.5 * np.exp(0.3 * n(H)) * u[:, 0]).astype(np.float32),
        "tab2_words": tab2_words, "tab2_scales": tab2_scales,
        "offs2": striped(np.random.permutation(T3)[:S2]),
        "prior": (0.8 * n((S2, S))).astype(np.float32),
        "emph": (0.5 * np.exp(0.4 * n(S2))).astype(np.float32),
        "offs3": striped(np.random.permutation(T2)[:S]),
        "wgo": np.exp(0.3 * n((128, S))).astype(np.float32),
        "page1": (0.6 * n((S2, T2))).astype(np.float32),
    }

def reference(tab_words, tab_scales, offs, w1, w2, w3_words, w3_scales, gain, tab2_words, tab2_scales, offs2, prior, emph, offs3, wgo, page1):
    v = unpack_weight(tab_words, tab_scales, "e4m3")[:, unstriped(offs)]
    v2 = unpack_weight(tab2_words, tab2_scales, "e4m3")[:, unstriped(offs2)]
    w3 = unpack_weight(w3_words, w3_scales, "e2m1")
    form = np.tanh(mxq(f64(w1), 0, "e4m3").T @ v)
    rhythm = np.sin(mxq(f64(w2), 0, "e4m3").T @ v)
    look = w3.T @ v
    h = np.maximum(f64(gain)[:, None] * (form + rhythm), look)
    hq = mxq(h, 0, "e4m3")
    e = v2.T @ hq + v2.T @ v
    y = f64(emph)[:, None] * (e + f64(prior))
    out = f64(page1).copy()
    out[:, unstriped(offs3)] = np.tile(f64(wgo), (S2 // 128, 1)) * y
    return out

@@ -1,0 +1,322 @@
+import math
+from contextlib import ExitStack
+
+import concourse.mybir as mybir
+from concourse.masks import make_identity
+
+K, T, S, H, T3, S2, T2 = 1024, 2048, 512, 1024, 2048, 512, 1024
+FLOPS = 2 * (3 * K * H * S + 2 * H * S2 * S)
+
+F32 = mybir.dt.float32
+BF16 = mybir.dt.bfloat16
+I32 = mybir.dt.int32
+U32 = mybir.dt.uint32
+U16 = mybir.dt.uint16
+U8 = mybir.dt.uint8
+FP8X4 = mybir.dt.float8_e4m3fn_x4
+FP4X4 = mybir.dt.float4_e2m1fn_x4
+ALU = mybir.AluOpType
+ACT = mybir.ActivationFunctionType
+
+P = 128
+PACK = 4
+KP = P * PACK
+PASSES = K // KP
+JB = S // P
+MB = S2 // P
+HALF = S // 2
+TWO_PI = 2.0 * math.pi
+W2_PIECES = [(0, 256), (256, 512), (512, 1024)]
+W1_PIECES = [(0, 512), (512, 768), (768, 1024)]
+
+
+def tile_list_netball_selection_page_kernel(
+    tc, tab_words, tab_scales, offs, w1, w2, w3_words, w3_scales, gain, tab2_words, tab2_scales,
+    offs2, prior, emph, offs3, wgo, page1, out,
+):
+    nc = tc.nc
+    with ExitStack() as ctx:
+        keep = ctx.enter_context(tc.tile_pool(name="keep", bufs=1))
+        ring = ctx.enter_context(tc.tile_pool(name="ring", bufs=2))
+        psum = ctx.enter_context(tc.psum_pool(name="psum", bufs=1))
+        banks = [psum.tile([P, KP], F32, name=f"bank{n}") for n in range(8)]
+
+        idx = keep.tile([P, S // 16], U16, name="idx")
+        idx2 = keep.tile([P, S2 // 16], U16, name="idx2")
+        idx3 = keep.tile([P, S // 16], U16, name="idx3")
+        gain_sb = keep.tile([P, PASSES, PACK], F32, name="gain_sb")
+        emph_sb = keep.tile([P, MB], F32, name="emph_sb")
+        ident = keep.tile([P, P], F32, name="ident")
+
+        tabw = [keep.tile([P, T], I32, name=f"tabw{a}", align_bytes=64) for a in range(PASSES)]
+        tab2w = [keep.tile([P, T3], I32, name=f"tab2w{a}", align_bytes=64) for a in range(PASSES)]
+        tabs = keep.tile([P, T], U8, name="tabs", align_bytes=64)
+        tab2s = keep.tile([P, T3], U8, name="tab2s", align_bytes=64)
+        w3w = keep.tile([P, PASSES, 2 * H], U8, name="w3w", align_bytes=64)
+        w3s = keep.tile([P, H], U8, name="w3s", align_bytes=64)
+        w3wp = keep.tile([P, PASSES, 2 * H], U8, name="w3wp", align_bytes=64)
+        w3sp = [keep.tile([P, H], U8, name=f"w3sp{a}", align_bytes=64) for a in range(PASSES)]
+        vw = [keep.tile([P, S], U32, name=f"vw{a}", align_bytes=64) for a in range(PASSES)]
+        vs = keep.tile([P, S], U8, name="vs", align_bytes=64)
+        vs_low = keep.tile([P, S], U8, name="vs_low", align_bytes=64)
+        v2w = [keep.tile([P, S2], U32, name=f"v2w{a}", align_bytes=64) for a in range(PASSES)]
+        v2s = keep.tile([P, S2], U8, name="v2s", align_bytes=64)
+        weights = {"w1": w1, "w2": w2}
+        pieces = {"w1": W1_PIECES, "w2": W2_PIECES}
+        raw = {}
+        codes = {}
+        for name in ("w2", "w1"):
+            for n, (c0, c1) in enumerate(pieces[name]):
+                for a in range(PASSES):
+                    raw[name, n, a] = keep.tile([P, PACK, c1 - c0], F32, name=f"raw_{name}{n}{a}", tag=f"raw_{name}{n}{a}")
+                    codes[name, n, a] = (
+                        keep.tile([P, c1 - c0], U32, name=f"wc_{name}{n}{a}", align_bytes=64),
+                        keep.tile([P, c1 - c0], U8, name=f"ws_{name}{n}{a}", align_bytes=64),
+                    )
+        wgo_sb = keep.tile([P, S], F32, name="wgo_sb")
+        prior_sb = [keep.tile([P, S], F32, name=f"prior{m}") for m in range(MB)]
+        weight = [raw["w2", 0, m // 2][:].rearrange("p j c -> p (j c)")[:, (m % 2) * S:(m % 2 + 1) * S] for m in range(MB)]
+        page = [keep.tile([P, T2], F32, name=f"page{m}") for m in range(MB)]
+        frac = {}
+        for b in range(PASSES):
+            for jb in range(JB):
+                frac[b, jb] = keep.tile([P, PACK, P], F32, name=f"frac_{b}{jb}")
+        hc = [keep.tile([P, S], U32, name=f"hc{b}", align_bytes=64) for b in range(PASSES)]
+        hs = [keep.tile([P, S], U8, name=f"hs{b}", align_bytes=64) for b in range(PASSES)]
+
+        for plane in (tabs, w3s, tab2s, vs_low, w3sp[1]):
+            nc.vector.memset(plane[:].bitcast(I32), 0)
+        make_identity(nc, ident[:])
+
+        def load_w(name, n):
+            c0, c1 = pieces[name][n]
+            for a in range(PASSES):
+                src = weights[name][a * KP:(a + 1) * KP, c0:c1]
+                nc.sync.dma_start(out=raw[name, n, a][:], in_=src.rearrange("(p j) c -> p j c", j=PACK))
+
+        def load_words(dst, src, a):
+            nc.sync.dma_start(out=dst[a][:], in_=src[a].rearrange("p t i -> p (t i)").bitcast(I32))
+
+        def load_planes(dst, src):
+            for q in range(4):
+                nc.sync.dma_start(
+                    out=dst[32 * q:32 * q + 4 * PASSES, :].bitcast(I32),
+                    in_=src[:, 4 * q:4 * q + 4, :].bitcast(I32),
+                )
+
+        def lower_plane(dst, src):
+            nc.sync.dma_start(out=dst[0:P - 4, :].bitcast(I32), in_=src[4:P, :].bitcast(I32))
+
+        cast_engine = {"w100":"v","w110":"v","w121":"v"}
+        kept = {}
+        kgate = {"12":"w220","13":"w220b","22":"w101","23":"w111"}
+
+        def quantize_w(name, n, a):
+            c0, c1 = pieces[name][n]
+            key = f"{name}{n}{a}"
+            if key in [v[0:4] for v in kgate.values()]:
+                grouped = keep.tile([P, (c1 - c0) * PACK], BF16, name="g_" + key, align_bytes=64)
+                kept[key] = grouped
+            else:
+                grouped = ring.tile([P, (c1 - c0) * PACK], BF16, name="grouped", bufs=3, align_bytes=64)
+            engine = cast_engine.get(key, "s")
+            step = 128 if engine == "g" else c1 - c0
+            for d0 in range(0, c1 - c0, step):
+                dst = grouped[:, d0 * PACK:(d0 + step) * PACK].rearrange("p (c i j) -> p c j i", i=4, j=PACK)
+                src = raw[name, n, a][:, :, d0:d0 + step].rearrange("p j (c i) -> p c j i", i=4)
+                if engine == "s":
+                    nc.scalar.copy(out=dst, in_=src)
+                elif engine == "g":
+                    nc.gpsimd.tensor_scalar(dst, src, 1.0, 0.0, ALU.mult, ALU.add)
+                else:
+                    nc.vector.tensor_copy(out=dst, in_=src)
+            wc, ws = codes[name, n, a]
+            nc.vector.quantize_mx(out=wc[:].bitcast(FP8X4), scales=ws[:], in_=grouped[:])
+
+        def product(name, ns, jb, x):
+            cols = slice(jb * P, (jb + 1) * P)
+            base = pieces[name][ns[0]][0]
+            for n in ns:
+                c0, c1 = pieces[name][n]
+                for a in range(PASSES):
+                    wc, ws = codes[name, n, a]
+                    nc.tensor.matmul_mx(
+                        out=x[:, c0 - base:c1 - base], lhsT=vw[a][:, cols].bitcast(FP8X4), lhsT_scale=vs[4 * a:P, cols],
+                        rhs=wc[:].bitcast(FP8X4), rhs_scale=ws[:], start=(a == 0), stop=(a == PASSES - 1),
+                    )
+            width = pieces[name][ns[-1]][1] - base
+            return x[:, 0:width].rearrange("p (m t) -> p t m", t=PACK), base // KP, slice((base % KP) // PACK, (base % KP + width) // PACK)
+
+        def reduce_angle(ns, jb, bank):
+            x, b, ms = product("w2", ns, jb, bank)
+            key = f"{ns[0]}{jb}"
+            if key in kgate:
+                width = PACK * (ms.stop - ms.start)
+                first = 2 * width if len(kgate[key]) == 5 else 0
+                turns = kept[kgate[key][0:4]][:, first:first + 2 * width].bitcast(I32).rearrange("p (t m) -> p t m", t=PACK)
+            else:
+                turns = ring.tile([P, PACK, ms.stop - ms.start], I32, name="turns")
+            nc.vector.tensor_scalar(turns[:], x, 1.0 / TWO_PI, None, ALU.mult)
+            nc.vector.scalar_tensor_tensor(frac[b, jb][:, :, ms], x, 1.0 / TWO_PI, turns[:], ALU.mult, ALU.subtract)
+
+        wave = {}
+
+        def sines(b, jbs, host):
+            waves = host[:].rearrange("p j c -> p (j c)").rearrange("p (n t m) -> p n t m", t=PACK, m=P)
+            for n, jb in enumerate(jbs):
+                wave[b, jb] = waves[:, n]
+                nc.scalar.activation(waves[:, n], frac[b, jb][:], ACT.Sin, scale=TWO_PI)
+
+        forms = {}
+
+        def form_of(ns, jb):
+            x, b, ms = product("w1", ns, jb, banks[jb % 2])
+            if (b, jb) not in forms:
+                forms[b, jb] = ring.tile([P, PACK, P], F32, name="form", bufs=3)
+            nc.scalar.activation(forms[b, jb][:, :, ms], x, ACT.Tanh)
+
+        hb = {}
+
+        def features(b, jb):
+            both = banks[2 + jb % 2][:].rearrange("p (t j) -> p t j", t=PACK)
+            for t in range(PACK):
+                nc.tensor.matmul(both[:, t, :], forms[b, jb][:, t, :], ident[:], start=True, stop=False, is_transpose=True)
+                nc.tensor.matmul(both[:, t, :], wave[b, jb][:, t, :], ident[:], start=False, stop=True, is_transpose=True)
+            look = banks[4 + jb % 2][:].rearrange("p (t j) -> p t j", t=PACK)
+            cols = slice(jb * P, (jb + 1) * P)
+            planes = (vs, vs_low)
+            for t in range(PACK):
+                c0 = b * KP + t * P
+                for a in range(PASSES):
+                    nc.tensor.matmul_mx(
+                        out=look[:, t, :], lhsT=w3wp[:, a, 2 * c0:2 * (c0 + P)].bitcast(FP4X4),
+                        lhsT_scale=w3sp[a][:, c0:c0 + P],
+                        rhs=vw[a][:, cols].bitcast(FP8X4), rhs_scale=planes[a][:, cols],
+                        start=(a == 0), stop=(a == PASSES - 1),
+                    )
+            gained = ring.tile([P, PACK, P], F32, name="gained")
+            for t in range(PACK):
+                nc.scalar.activation(gained[:, t, :], both[:, t, :], ACT.Copy, scale=gain_sb[:, b, t:t + 1])
+            half, within = divmod(jb, 2)
+            if within == 0:
+                hb[b, half] = ring.tile([P, HALF * PACK], BF16, name="hb", align_bytes=64)
+            nc.vector.tensor_tensor(
+                hb[b, half][:, within * KP:(within + 1) * KP].rearrange("p (c i t) -> p c t i", i=4, t=PACK),
+                look[:].rearrange("p t (c i) -> p c t i", i=4),
+                gained[:].rearrange("p t (c i) -> p c t i", i=4),
+                ALU.max,
+            )
+
+        def quantize_h(b, half):
+            cols = slice(half * HALF, (half + 1) * HALF)
+            nc.vector.quantize_mx(out=hc[b][:, cols].bitcast(FP8X4), scales=hs[b][:, cols], in_=hb[b, half][:])
+
+        def scores(m, half):
+            rows = slice(m * P, (m + 1) * P)
+            cols = slice(half * HALF, (half + 1) * HALF)
+            e = banks[6 + m % 2][:, 0:HALF]
+            movers = [(a, vw[a], vs[4 * a:P, cols]) for a in range(PASSES)] + [(b, hc[b], hs[b][:, cols]) for b in range(PASSES)]
+            for n, (a, words, plane) in enumerate(movers):
+                nc.tensor.matmul_mx(
+                    out=e[:], lhsT=v2w[a][:, rows].bitcast(FP8X4), lhsT_scale=v2s[4 * a:P, rows],
+                    rhs=words[:, cols].bitcast(FP8X4), rhs_scale=plane,
+                    start=(n == 0), stop=(n == len(movers) - 1),
+                )
+            score = ring.tile([P, HALF], F32, name="score")
+            nc.vector.tensor_tensor(score[:], e[:], prior_sb[m][:, cols], ALU.add)
+            entries = slice(half * HALF // 16, (half + 1) * HALF // 16)
+            nc.vector.tensor_tensor(page[m][:].indirect(idx3[:, entries]), score[:], weight[m][:, cols], ALU.mult)
+            if half == 1:
+                nc.sync.dma_start(out=out[rows, :], in_=page[m][:])
+
+        def permute_w3_words():
+            for a in range(PASSES):
+                nc.vector.tensor_copy(
+                    out=w3wp[:, a, :].bitcast(U16).rearrange("p (b t m) -> p b t m", b=PASSES, t=PACK),
+                    in_=w3w[:, a, :].bitcast(U16).rearrange("p (b m t) -> p b t m", b=PASSES, t=PACK),
+                )
+
+        def permute_w3_scales():
+            nc.vector.tensor_copy(
+                out=w3sp[0][:].rearrange("p (b t m) -> p b t m", b=PASSES, t=PACK),
+                in_=w3s[:].rearrange("p (b m t) -> p b t m", b=PASSES, t=PACK),
+            )
+            lower_plane(w3sp[1], w3sp[0])
+
+        load_words(tabw, tab_words, 0)
+        nc.sync.dma_start(idx[:], offs)
+        nc.sync.dma_start(out=gain_sb[:], in_=gain.rearrange("(b p t) -> p b t", b=PASSES, t=PACK))
+        with nc.allow_non_contiguous_dma(reason="one emphasis value a row of the page"):
+            nc.sync.dma_start(out=emph_sb[:], in_=emph.rearrange("(m p) -> p m", p=P))
+        load_w("w2", 0)
+        nc.sync.dma_start(idx2[:], offs2)
+        nc.sync.dma_start(idx3[:], offs3)
+        load_planes(tabs, tab_scales)
+        load_words(tabw, tab_words, 1)
+        load_w("w2", 1)
+        nc.sync.dma_start(out=w3w[:].bitcast(I32), in_=w3_words.rearrange("a p c -> p a c").bitcast(I32))
+        load_planes(w3s, w3_scales)
+
+        nc.vector.tensor_copy(vw[0][:], tabw[0][:].bitcast(U32).indirect(idx[:]))
+        nc.vector.tensor_copy(vs[:], tabs[:].indirect(idx[:]))
+        quantize_w("w2", 0, 0)
+        quantize_w("w2", 0, 1)
+        nc.vector.tensor_copy(vw[1][:], tabw[1][:].bitcast(U32).indirect(idx[:]))
+
+        load_w("w2", 2)
+        load_w("w1", 0)
+        load_planes(tab2s, tab2_scales)
+        lower_plane(vs_low, vs)
+        quantize_w("w2", 1, 0)
+        quantize_w("w2", 1, 1)
+        quantize_w("w2", 2, 0)
+        quantize_w("w2", 2, 1)
+        for n in (0, 1):
+            for jb in range(JB):
+                reduce_angle([n], jb, banks[JB * n + jb])
+        load_w("w1", 1)
+        permute_w3_words()
+        permute_w3_scales()
+        load_w("w1", 2)
+        load_words(tab2w, tab2_words, 0)
+        load_words(tab2w, tab2_words, 1)
+        nc.sync.dma_start(out=wgo_sb[:], in_=wgo)
+        for m in range(MB):
+            nc.sync.dma_start(out=prior_sb[m][:], in_=prior[m * P:(m + 1) * P, :])
+            nc.sync.dma_start(out=page[m][:], in_=page1[m * P:(m + 1) * P, :])
+        for n in range(3):
+            for a in range(PASSES):
+                quantize_w("w1", n, a)
+        for jb in range(JB):
+            reduce_angle([2], jb, banks[JB + jb])
+        sines(0, (0, 1, 2, 3), raw["w2", 2, 1])
+        sines(1, (0, 1), raw["w1", 0, 1])
+        for m in range(MB):
+            nc.scalar.activation(weight[m][:], wgo_sb[:], ACT.Copy, scale=emph_sb[:, m:m + 1])
+        for jb in (0, 1):
+            form_of([0], jb)
+            features(0, jb)
+        for jb in (0, 1):
+            form_of([1, 2], jb)
+        quantize_h(0, 0)
+        for jb in (0, 1):
+            features(1, jb)
+        quantize_h(1, 0)
+        nc.vector.tensor_copy(v2s[:], tab2s[:].indirect(idx2[:]))
+        for a in range(PASSES):
+            nc.vector.tensor_copy(v2w[a][:], tab2w[a][:].bitcast(U32).indirect(idx2[:]))
+        scores(0, 0)
+        for jb in (2, 3):
+            form_of([0], jb)
+            features(0, jb)
+        scores(1, 0)
+        quantize_h(0, 1)
+        sines(1, (2, 3), raw["w1", 2, 1])
+        for jb in (2, 3):
+            form_of([1, 2], jb)
+            features(1, jb)
+        scores(2, 0)
+        quantize_h(1, 1)
+        scores(3, 0)
+        for m in range(MB):
+            scores(m, 1)

@@ -68,14 +68,14 @@ def tile_list_netball_selection_page_kernel(
         for name in ("w2", "w1"):
             for n, (c0, c1) in enumerate(pieces[name]):
                 for a in range(PASSES):
-                    raw[name, n, a] = keep.tile([P, PACK, c1 - c0], F32, name=f"raw_{name}{n}{a}", tag=f"raw_{name}{n}{a}")
+                    raw[name, n, a] = keep.tile([P, PACK * (c1 - c0)], F32, name=f"raw_{name}{n}{a}", align_bytes=64)
                     codes[name, n, a] = (
                         keep.tile([P, c1 - c0], U32, name=f"wc_{name}{n}{a}", align_bytes=64),
                         keep.tile([P, c1 - c0], U8, name=f"ws_{name}{n}{a}", align_bytes=64),
                     )
         wgo_sb = keep.tile([P, S], F32, name="wgo_sb")
         prior_sb = [keep.tile([P, S], F32, name=f"prior{m}") for m in range(MB)]
-        weight = [raw["w2", 0, m // 2][:].rearrange("p j c -> p (j c)")[:, (m % 2) * S:(m % 2 + 1) * S] for m in range(MB)]
+        weight = [raw["w2", 0, m // 2][:, (m % 2) * S:(m % 2 + 1) * S] for m in range(MB)]
         page = [keep.tile([P, T2], F32, name=f"page{m}") for m in range(MB)]
         frac = {}
         for b in range(PASSES):
@@ -83,16 +83,24 @@ def tile_list_netball_selection_page_kernel(
                 frac[b, jb] = keep.tile([P, PACK, P], F32, name=f"frac_{b}{jb}")
         hc = [keep.tile([P, S], U32, name=f"hc{b}", align_bytes=64) for b in range(PASSES)]
         hs = [keep.tile([P, S], U8, name=f"hs{b}", align_bytes=64) for b in range(PASSES)]
+        staging = [keep.tile([P, KP * PACK], BF16, name=f"staging{n}", align_bytes=64) for n in range(3)]
 
-        for plane in (tabs, w3s, tab2s, vs_low, w3sp[1]):
-            nc.vector.memset(plane[:].bitcast(I32), 0)
+        for plane in (w3s, tabs, tab2s, vs_low, w3sp[1]):
+            nc.gpsimd.memset(plane[:].bitcast(I32), 0)
         make_identity(nc, ident[:])
+        warm = keep.tile([P, 1], F32, name="warm")
+        nc.scalar.activation(warm[:], ident[:, 0:1], ACT.Silu)
+
+        def load_w_pass(name, n, a):
+            c0, c1 = pieces[name][n]
+            src = weights[name][a * KP:(a + 1) * KP, c0:c1]
+            nc.sync.dma_start(
+                out=raw[name, n, a][:].rearrange("p (j c) -> p j c", j=PACK), in_=src.rearrange("(p j) c -> p j c", j=PACK)
+            )
 
         def load_w(name, n):
-            c0, c1 = pieces[name][n]
             for a in range(PASSES):
-                src = weights[name][a * KP:(a + 1) * KP, c0:c1]
-                nc.sync.dma_start(out=raw[name, n, a][:], in_=src.rearrange("(p j) c -> p j c", j=PACK))
+                load_w_pass(name, n, a)
 
         def load_words(dst, src, a):
             nc.sync.dma_start(out=dst[a][:], in_=src[a].rearrange("p t i -> p (t i)").bitcast(I32))
@@ -107,33 +115,30 @@ def tile_list_netball_selection_page_kernel(
         def lower_plane(dst, src):
             nc.sync.dma_start(out=dst[0:P - 4, :].bitcast(I32), in_=src[4:P, :].bitcast(I32))
 
-        cast_engine = {"w100":"v","w110":"v","w121":"v"}
-        kept = {}
-        kgate = {"12":"w220","13":"w220b","22":"w101","23":"w111"}
+        grouped = {}
 
-        def quantize_w(name, n, a):
+        def cast(name, n, a, engine, lo, hi):
             c0, c1 = pieces[name][n]
-            key = f"{name}{n}{a}"
-            if key in [v[0:4] for v in kgate.values()]:
-                grouped = keep.tile([P, (c1 - c0) * PACK], BF16, name="g_" + key, align_bytes=64)
-                kept[key] = grouped
+            if (name, n, a) not in grouped:
+                grouped[name, n, a] = staging[len(grouped) % 3][:, 0:(c1 - c0) * PACK]
+            d0, d1 = (c1 - c0) * lo // 8, (c1 - c0) * hi // 8
+            dst = grouped[name, n, a][:, d0 * PACK:d1 * PACK].rearrange("p (c i j) -> p c j i", i=4, j=PACK)
+            src = raw[name, n, a][:].rearrange("p (j c) -> p j c", j=PACK)[:, :, d0:d1].rearrange("p j (c i) -> p c j i", i=4)
+            if engine == "s":
+                nc.scalar.copy(out=dst, in_=src)
+            elif engine == "g":
+                nc.gpsimd.tensor_scalar(dst, src, 1.0, 0.0, ALU.mult, ALU.add)
             else:
-                grouped = ring.tile([P, (c1 - c0) * PACK], BF16, name="grouped", bufs=3, align_bytes=64)
-            engine = cast_engine.get(key, "s")
-            step = 128 if engine == "g" else c1 - c0
-            for d0 in range(0, c1 - c0, step):
-                dst = grouped[:, d0 * PACK:(d0 + step) * PACK].rearrange("p (c i j) -> p c j i", i=4, j=PACK)
-                src = raw[name, n, a][:, :, d0:d0 + step].rearrange("p j (c i) -> p c j i", i=4)
-                if engine == "s":
-                    nc.scalar.copy(out=dst, in_=src)
-                elif engine == "g":
-                    nc.gpsimd.tensor_scalar(dst, src, 1.0, 0.0, ALU.mult, ALU.add)
-                else:
-                    nc.vector.tensor_copy(out=dst, in_=src)
-            wc, ws = codes[name, n, a]
-            nc.vector.quantize_mx(out=wc[:].bitcast(FP8X4), scales=ws[:], in_=grouped[:])
+                nc.vector.tensor_copy(out=dst, in_=src)
 
-        def product(name, ns, jb, x):
+        def quant(name, n, a):
+            wc, ws = codes[name, n, a]
+            nc.vector.quantize_mx(out=wc[:].bitcast(FP8X4), scales=ws[:], in_=grouped[name, n, a])
+
+        sums = {}
+
+        def product(name, ns, jb, bank):
+            x = banks[bank]
             cols = slice(jb * P, (jb + 1) * P)
             base = pieces[name][ns[0]][0]
             for n in ns:
@@ -145,96 +150,129 @@ def tile_list_netball_selection_page_kernel(
                         rhs=wc[:].bitcast(FP8X4), rhs_scale=ws[:], start=(a == 0), stop=(a == PASSES - 1),
                     )
             width = pieces[name][ns[-1]][1] - base
-            return x[:, 0:width].rearrange("p (m t) -> p t m", t=PACK), base // KP, slice((base % KP) // PACK, (base % KP + width) // PACK)
+            sums[name, ns[0], jb] = (
+                x[:, 0:width].rearrange("p (m t) -> p t m", t=PACK), base // KP,
+                slice((base % KP) // PACK, (base % KP + width) // PACK),
+            )
 
-        def reduce_angle(ns, jb, bank):
-            x, b, ms = product("w2", ns, jb, bank)
-            key = f"{ns[0]}{jb}"
-            if key in kgate:
-                width = PACK * (ms.stop - ms.start)
-                first = 2 * width if len(kgate[key]) == 5 else 0
-                turns = kept[kgate[key][0:4]][:, first:first + 2 * width].bitcast(I32).rearrange("p (t m) -> p t m", t=PACK)
+        turns = {}
+
+        def count_turns(n, jb, host=None):
+            x, b, ms = sums["w2", n, jb]
+            if host is None:
+                turns[n, jb] = ring.tile([P, PACK, ms.stop - ms.start], I32, name="turns", bufs=3)[:]
             else:
-                turns = ring.tile([P, PACK, ms.stop - ms.start], I32, name="turns")
-            nc.vector.tensor_scalar(turns[:], x, 1.0 / TWO_PI, None, ALU.mult)
-            nc.vector.scalar_tensor_tensor(frac[b, jb][:, :, ms], x, 1.0 / TWO_PI, turns[:], ALU.mult, ALU.subtract)
+                turns[n, jb] = host.bitcast(I32)[:, 0:PACK * (ms.stop - ms.start)].rearrange("p (t m) -> p t m", t=PACK)
+            nc.vector.tensor_scalar(turns[n, jb], x, 1.0 / TWO_PI, None, ALU.mult)
+
+        def fraction(n, jb):
+            x, b, ms = sums["w2", n, jb]
+            nc.vector.scalar_tensor_tensor(frac[b, jb][:, :, ms], x, 1.0 / TWO_PI, turns[n, jb], ALU.mult, ALU.subtract)
 
         wave = {}
 
-        def sines(b, jbs, host):
-            waves = host[:].rearrange("p j c -> p (j c)").rearrange("p (n t m) -> p n t m", t=PACK, m=P)
-            for n, jb in enumerate(jbs):
-                wave[b, jb] = waves[:, n]
-                nc.scalar.activation(waves[:, n], frac[b, jb][:], ACT.Sin, scale=TWO_PI)
+        def sine(b, jb, host, slot):
+            wave[b, jb] = host[:, slot * KP:(slot + 1) * KP].rearrange("p (t m) -> p t m", t=PACK)
+            nc.scalar.activation(wave[b, jb], frac[b, jb][:], ACT.Sin, scale=TWO_PI)
 
         forms = {}
 
-        def form_of(ns, jb):
-            x, b, ms = product("w1", ns, jb, banks[jb % 2])
+        def tanh(n, jb):
+            x, b, ms = sums["w1", n, jb]
             if (b, jb) not in forms:
                 forms[b, jb] = ring.tile([P, PACK, P], F32, name="form", bufs=3)
             nc.scalar.activation(forms[b, jb][:, :, ms], x, ACT.Tanh)
 
-        hb = {}
+        looks = {}
 
-        def features(b, jb):
-            both = banks[2 + jb % 2][:].rearrange("p (t j) -> p t j", t=PACK)
-            for t in range(PACK):
-                nc.tensor.matmul(both[:, t, :], forms[b, jb][:, t, :], ident[:], start=True, stop=False, is_transpose=True)
-                nc.tensor.matmul(both[:, t, :], wave[b, jb][:, t, :], ident[:], start=False, stop=True, is_transpose=True)
-            look = banks[4 + jb % 2][:].rearrange("p (t j) -> p t j", t=PACK)
+        def look_of(b, jb, bank):
+            look = banks[bank][:].rearrange("p (t j) -> p t j", t=PACK)
+            looks[b, jb] = look
             cols = slice(jb * P, (jb + 1) * P)
             planes = (vs, vs_low)
             for t in range(PACK):
                 c0 = b * KP + t * P
-                for a in range(PASSES):
+                for n, a in enumerate((1, 0)):
                     nc.tensor.matmul_mx(
                         out=look[:, t, :], lhsT=w3wp[:, a, 2 * c0:2 * (c0 + P)].bitcast(FP4X4),
                         lhsT_scale=w3sp[a][:, c0:c0 + P],
                         rhs=vw[a][:, cols].bitcast(FP8X4), rhs_scale=planes[a][:, cols],
-                        start=(a == 0), stop=(a == PASSES - 1),
+                        start=(n == 0), stop=(n == PASSES - 1),
                     )
-            gained = ring.tile([P, PACK, P], F32, name="gained")
+
+        boths = {}
+
+        def turn(b, jb, bank):
+            both = banks[bank][:].rearrange("p (t j) -> p t j", t=PACK)
+            boths[b, jb] = both
             for t in range(PACK):
-                nc.scalar.activation(gained[:, t, :], both[:, t, :], ACT.Copy, scale=gain_sb[:, b, t:t + 1])
+                nc.tensor.matmul(both[:, t, :], forms[b, jb][:, t, :], ident[:], start=True, stop=False, is_transpose=True)
+                nc.tensor.matmul(both[:, t, :], wave[b, jb][:, t, :], ident[:], start=False, stop=True, is_transpose=True)
+
+        gained = {}
+
+        def apply_gain(b, jb):
+            gained[b, jb] = ring.tile([P, PACK, P], F32, name="gained", bufs=3)
+            for t in range(PACK):
+                nc.scalar.activation(gained[b, jb][:, t, :], boths[b, jb][:, t, :], ACT.Copy, scale=gain_sb[:, b, t:t + 1])
+
+        hb = {}
+
+        def feature(b, jb):
             half, within = divmod(jb, 2)
             if within == 0:
                 hb[b, half] = ring.tile([P, HALF * PACK], BF16, name="hb", align_bytes=64)
             nc.vector.tensor_tensor(
                 hb[b, half][:, within * KP:(within + 1) * KP].rearrange("p (c i t) -> p c t i", i=4, t=PACK),
-                look[:].rearrange("p t (c i) -> p c t i", i=4),
-                gained[:].rearrange("p t (c i) -> p c t i", i=4),
+                looks[b, jb].rearrange("p t (c i) -> p c t i", i=4),
+                gained[b, jb][:].rearrange("p t (c i) -> p c t i", i=4),
                 ALU.max,
             )
 
-        def quantize_h(b, half):
+        def quant_h(b, half):
             cols = slice(half * HALF, (half + 1) * HALF)
             nc.vector.quantize_mx(out=hc[b][:, cols].bitcast(FP8X4), scales=hs[b][:, cols], in_=hb[b, half][:])
 
-        def scores(m, half):
+        es = {}
+
+        def meet(m, half, bank):
             rows = slice(m * P, (m + 1) * P)
             cols = slice(half * HALF, (half + 1) * HALF)
-            e = banks[6 + m % 2][:, 0:HALF]
+            e = banks[bank][:, 0:HALF]
+            es[m, half] = e
             movers = [(a, vw[a], vs[4 * a:P, cols]) for a in range(PASSES)] + [(b, hc[b], hs[b][:, cols]) for b in range(PASSES)]
             for n, (a, words, plane) in enumerate(movers):
                 nc.tensor.matmul_mx(
-                    out=e[:], lhsT=v2w[a][:, rows].bitcast(FP8X4), lhsT_scale=v2s[4 * a:P, rows],
+                    out=e, lhsT=v2w[a][:, rows].bitcast(FP8X4), lhsT_scale=v2s[4 * a:P, rows],
                     rhs=words[:, cols].bitcast(FP8X4), rhs_scale=plane,
                     start=(n == 0), stop=(n == len(movers) - 1),
                 )
-            score = ring.tile([P, HALF], F32, name="score")
-            nc.vector.tensor_tensor(score[:], e[:], prior_sb[m][:, cols], ALU.add)
-            entries = slice(half * HALF // 16, (half + 1) * HALF // 16)
-            nc.vector.tensor_tensor(page[m][:].indirect(idx3[:, entries]), score[:], weight[m][:, cols], ALU.mult)
-            if half == 1:
-                nc.sync.dma_start(out=out[rows, :], in_=page[m][:])
 
-        def permute_w3_words():
-            for a in range(PASSES):
-                nc.vector.tensor_copy(
-                    out=w3wp[:, a, :].bitcast(U16).rearrange("p (b t m) -> p b t m", b=PASSES, t=PACK),
-                    in_=w3w[:, a, :].bitcast(U16).rearrange("p (b m t) -> p b t m", b=PASSES, t=PACK),
-                )
+        score = {}
+
+        def add_prior(m, half):
+            cols = slice(half * HALF, (half + 1) * HALF)
+            score[m, half] = ring.tile([P, HALF], F32, name="score", bufs=3)
+            nc.vector.tensor_tensor(score[m, half][:], es[m, half], prior_sb[m][:, cols], ALU.add)
+
+        def place(m, half):
+            cols = slice(half * HALF, (half + 1) * HALF)
+            entries = slice(half * HALF // 16, (half + 1) * HALF // 16)
+            nc.vector.tensor_tensor(page[m][:].indirect(idx3[:, entries]), score[m, half][:], weight[m][:, cols], ALU.mult)
+            if half == 1:
+                nc.sync.dma_start(out=out[m * P:(m + 1) * P, :], in_=page[m][:])
+
+        def weigh(m, engine):
+            if engine == "g":
+                nc.gpsimd.tensor_scalar(weight[m], wgo_sb[:], emph_sb[:, m:m + 1], 0.0, ALU.mult, ALU.add)
+            else:
+                nc.scalar.activation(weight[m], wgo_sb[:], ACT.Copy, scale=emph_sb[:, m:m + 1])
+
+        def permute_w3_words(a):
+            nc.vector.tensor_copy(
+                out=w3wp[:, a, :].bitcast(U16).rearrange("p (b t m) -> p b t m", b=PASSES, t=PACK),
+                in_=w3w[:, a, :].bitcast(U16).rearrange("p (b m t) -> p b t m", b=PASSES, t=PACK),
+            )
 
         def permute_w3_scales():
             nc.vector.tensor_copy(
@@ -243,80 +281,200 @@ def tile_list_netball_selection_page_kernel(
             )
             lower_plane(w3sp[1], w3sp[0])
 
+        def gather_words(dst, src, by):
+            nc.vector.tensor_copy(dst[:], src[:].bitcast(U32).indirect(by[:]))
+
+        def gather_bytes(dst, src, by):
+            nc.vector.tensor_copy(dst[:], src[:].indirect(by[:]))
+
+        def load_small():
+            nc.sync.dma_start(idx[:], offs)
+            nc.sync.dma_start(out=gain_sb[:], in_=gain.rearrange("(b p t) -> p b t", b=PASSES, t=PACK))
+            with nc.allow_non_contiguous_dma(reason="one emphasis value a row of the page"):
+                nc.sync.dma_start(out=emph_sb[:], in_=emph.rearrange("(m p) -> p m", p=P))
+
+        def load_w3():
+            nc.sync.dma_start(out=w3w[:].bitcast(I32), in_=w3_words.rearrange("a p c -> p a c").bitcast(I32))
+
+        def load_page():
+            nc.sync.dma_start(out=wgo_sb[:], in_=wgo)
+            for m in range(MB):
+                nc.sync.dma_start(out=prior_sb[m][:], in_=prior[m * P:(m + 1) * P, :])
+                nc.sync.dma_start(out=page[m][:], in_=page1[m * P:(m + 1) * P, :])
+
         load_words(tabw, tab_words, 0)
         nc.sync.dma_start(idx[:], offs)
         nc.sync.dma_start(out=gain_sb[:], in_=gain.rearrange("(b p t) -> p b t", b=PASSES, t=PACK))
-        with nc.allow_non_contiguous_dma(reason="one emphasis value a row of the page"):
-            nc.sync.dma_start(out=emph_sb[:], in_=emph.rearrange("(m p) -> p m", p=P))
-        load_w("w2", 0)
-        nc.sync.dma_start(idx2[:], offs2)
-        nc.sync.dma_start(idx3[:], offs3)
-        load_planes(tabs, tab_scales)
-        load_words(tabw, tab_words, 1)
-        load_w("w2", 1)
-        nc.sync.dma_start(out=w3w[:].bitcast(I32), in_=w3_words.rearrange("a p c -> p a c").bitcast(I32))
         load_planes(w3s, w3_scales)
+        load_words(tabw, tab_words, 1)
+        load_planes(tabs, tab_scales)
+        load_w("w2", 0)
+        load_w("w2", 1)
 
-        nc.vector.tensor_copy(vw[0][:], tabw[0][:].bitcast(U32).indirect(idx[:]))
-        nc.vector.tensor_copy(vs[:], tabs[:].indirect(idx[:]))
-        quantize_w("w2", 0, 0)
-        quantize_w("w2", 0, 1)
-        nc.vector.tensor_copy(vw[1][:], tabw[1][:].bitcast(U32).indirect(idx[:]))
-
-        load_w("w2", 2)
-        load_w("w1", 0)
-        load_planes(tab2s, tab2_scales)
-        lower_plane(vs_low, vs)
-        quantize_w("w2", 1, 0)
-        quantize_w("w2", 1, 1)
-        quantize_w("w2", 2, 0)
-        quantize_w("w2", 2, 1)
-        for n in (0, 1):
-            for jb in range(JB):
-                reduce_angle([n], jb, banks[JB * n + jb])
-        load_w("w1", 1)
-        permute_w3_words()
+        gather_words(vw[0], tabw[0], idx)
         permute_w3_scales()
+        gather_words(vw[1], tabw[1], idx)
+        gather_bytes(vs, tabs, idx)
+        lower_plane(vs_low, vs)
+        load_w("w1", 0)
+        load_w_pass("w2", 2, 0)
+        load_w3()
+        load_w_pass("w2", 2, 1)
+        nc.sync.dma_start(idx2[:], offs2)
+        load_planes(tab2s, tab2_scales)
+        load_w("w1", 1)
         load_w("w1", 2)
         load_words(tab2w, tab2_words, 0)
         load_words(tab2w, tab2_words, 1)
-        nc.sync.dma_start(out=wgo_sb[:], in_=wgo)
-        for m in range(MB):
-            nc.sync.dma_start(out=prior_sb[m][:], in_=prior[m * P:(m + 1) * P, :])
-            nc.sync.dma_start(out=page[m][:], in_=page1[m * P:(m + 1) * P, :])
-        for n in range(3):
-            for a in range(PASSES):
-                quantize_w("w1", n, a)
+        nc.sync.dma_start(idx3[:], offs3)
+        with nc.allow_non_contiguous_dma(reason="one emphasis value a row of the page"):
+            nc.sync.dma_start(out=emph_sb[:], in_=emph.rearrange("(m p) -> p m", p=P))
+        load_page()
+        cast("w2", 0, 0, "s", 0, 8)
+        quant("w2", 0, 0)
+        cast("w2", 0, 1, "s", 0, 3)
+        cast("w2", 0, 1, "v", 3, 8)
+        quant("w2", 0, 1)
         for jb in range(JB):
-            reduce_angle([2], jb, banks[JB + jb])
-        sines(0, (0, 1, 2, 3), raw["w2", 2, 1])
-        sines(1, (0, 1), raw["w1", 0, 1])
+            product("w2", [0], jb, jb)
+        cast("w2", 1, 0, "s", 0, 8)
+        cast("w2", 1, 1, "s", 0, 8)
+        quant("w2", 1, 0)
+        count_turns(0, 0)
+        count_turns(0, 1)
+        quant("w2", 1, 1)
+        for jb in range(JB):
+            product("w2", [1], jb, 4 + jb)
+        fraction(0, 0)
+        fraction(0, 1)
+        cast("w1", 0, 0, "s", 0, 8)
+        count_turns(1, 0)
+        count_turns(1, 1)
+        fraction(1, 0)
+        fraction(1, 1)
+        count_turns(0, 2)
+        count_turns(0, 3)
+        quant("w1", 0, 0)
+        cast("w1", 0, 1, "s", 0, 8)
+        fraction(0, 2)
+        fraction(0, 3)
+        count_turns(1, 2)
+        count_turns(1, 3)
+        fraction(1, 2)
+        fraction(1, 3)
+        quant("w1", 0, 1)
+        product("w1", [0], 0, 0)
+        product("w1", [0], 1, 1)
+        sine(0, 0, raw["w1", 0, 1], 0)
+        sine(0, 1, raw["w1", 0, 1], 1)
+        permute_w3_words(1)
+        permute_w3_words(0)
+        cast("w2", 2, 0, "s", 0, 5)
+        cast("w2", 2, 0, "v", 5, 8)
+        tanh(0, 0)
+        quant("w2", 2, 0)
+        turn(0, 0, 2)
+        look_of(0, 0, 4)
+        cast("w2", 2, 1, "s", 0, 5)
+        cast("w2", 2, 1, "v", 5, 8)
+        tanh(0, 1)
+        gather_bytes(v2s, tab2s, idx2)
+        quant("w2", 2, 1)
+        product("w2", [2], 0, 0)
+        turn(0, 1, 3)
+        product("w2", [2], 1, 1)
+        look_of(0, 1, 5)
+        look_of(1, 0, 6)
+        look_of(1, 1, 7)
+        cast("w1", 1, 0, "s", 0, 8)
+        quant("w1", 1, 0)
+        cast("w1", 1, 1, "s", 0, 8)
+        apply_gain(0, 0)
+        count_turns(2, 0)
+        quant("w1", 1, 1)
+        cast("w1", 2, 0, "s", 0, 8)
+        fraction(2, 0)
+        quant("w1", 2, 0)
+        cast("w1", 2, 1, "s", 0, 3)
+        cast("w1", 2, 1, "v", 3, 8)
+        count_turns(2, 1)
+        quant("w1", 2, 1)
+        apply_gain(0, 1)
+        product("w1", [1, 2], 0, 2)
+        fraction(2, 1)
+        feature(0, 0)
+        sine(1, 0, raw["w2", 2, 1], 0)
+        product("w1", [1, 2], 1, 3)
+        product("w2", [2], 2, 0)
+        product("w2", [2], 3, 1)
+        tanh(1, 0)
+        feature(0, 1)
+        gather_words(v2w[0], tab2w[0], idx2)
+        sine(1, 1, raw["w2", 2, 1], 1)
+        tanh(1, 1)
+        turn(1, 0, 4)
+        turn(1, 1, 5)
+        quant_h(0, 0)
+        count_turns(2, 2)
+        apply_gain(1, 0)
+        apply_gain(1, 1)
+        product("w1", [0], 2, 2)
+        product("w1", [0], 3, 3)
+        gather_words(v2w[1], tab2w[1], idx2)
+        feature(1, 0)
+        feature(1, 1)
+        fraction(2, 2)
+        quant_h(1, 0)
+        count_turns(2, 3)
+        weigh(0, "s")
+        meet(0, 0, 6)
+        meet(1, 0, 7)
+        fraction(2, 3)
+        sine(0, 2, raw["w1", 2, 1], 0)
+        tanh(0, 2)
+        sine(0, 3, raw["w1", 2, 1], 1)
+        tanh(0, 3)
+        turn(0, 2, 4)
+        look_of(0, 2, 0)
+        turn(0, 3, 5)
+        look_of(0, 3, 1)
+        product("w1", [1, 2], 2, 2)
+        product("w1", [1, 2], 3, 3)
+        weigh(1, "s")
+        apply_gain(0, 2)
+        sine(1, 2, raw["w1", 2, 0], 0)
+        apply_gain(0, 3)
+        add_prior(0, 0)
+        add_prior(1, 0)
+        place(0, 0)
+        meet(2, 0, 6)
+        meet(3, 0, 7)
+        weigh(2, "s")
+        tanh(1, 2)
+        sine(1, 3, raw["w1", 2, 0], 1)
+        tanh(1, 3)
+        weigh(3, "s")
+        place(1, 0)
+        feature(0, 2)
+        feature(0, 3)
+        turn(1, 2, 4)
+        look_of(1, 2, 0)
+        turn(1, 3, 5)
+        look_of(1, 3, 1)
+        add_prior(2, 0)
+        quant_h(0, 1)
+        apply_gain(1, 2)
+        apply_gain(1, 3)
+        place(2, 0)
+        add_prior(3, 0)
+        feature(1, 2)
+        feature(1, 3)
+        quant_h(1, 1)
+        place(3, 0)
         for m in range(MB):
-            nc.scalar.activation(weight[m][:], wgo_sb[:], ACT.Copy, scale=emph_sb[:, m:m + 1])
-        for jb in (0, 1):
-            form_of([0], jb)
-            features(0, jb)
-        for jb in (0, 1):
-            form_of([1, 2], jb)
-        quantize_h(0, 0)
-        for jb in (0, 1):
-            features(1, jb)
-        quantize_h(1, 0)
-        nc.vector.tensor_copy(v2s[:], tab2s[:].indirect(idx2[:]))
-        for a in range(PASSES):
-            nc.vector.tensor_copy(v2w[a][:], tab2w[a][:].bitcast(U32).indirect(idx2[:]))
-        scores(0, 0)
-        for jb in (2, 3):
-            form_of([0], jb)
-            features(0, jb)
-        scores(1, 0)
-        quantize_h(0, 1)
-        sines(1, (2, 3), raw["w1", 2, 1])
-        for jb in (2, 3):
-            form_of([1, 2], jb)
-            features(1, jb)
-        scores(2, 0)
-        quantize_h(1, 1)
-        scores(3, 0)
+            meet(m, 1, (6, 7, 2, 3)[m])
+        add_prior(0, 1)
         for m in range(MB):
-            scores(m, 1)
+            if m + 1 < MB:
+                add_prior(m + 1, 1)
+            place(m, 1)

@@ -45,8 +45,6 @@ def tile_list_netball_selection_page_kernel(
         idx2 = keep.tile([P, S2 // 16], U16, name="idx2")
         idx3 = keep.tile([P, S // 16], U16, name="idx3")
         gain_sb = keep.tile([P, PASSES, PACK], F32, name="gain_sb")
-        emph_sb = keep.tile([P, MB], F32, name="emph_sb")
-        ident = keep.tile([P, P], F32, name="ident")
 
         tabw = [keep.tile([P, T], I32, name=f"tabw{a}", align_bytes=64) for a in range(PASSES)]
         tab2w = [keep.tile([P, T3], I32, name=f"tab2w{a}", align_bytes=64) for a in range(PASSES)]
@@ -73,6 +71,8 @@ def tile_list_netball_selection_page_kernel(
                         keep.tile([P, c1 - c0], U32, name=f"wc_{name}{n}{a}", align_bytes=64),
                         keep.tile([P, c1 - c0], U8, name=f"ws_{name}{n}{a}", align_bytes=64),
                     )
+        ident = keep.tile([P, P], F32, name="ident")[:]
+        emph_sb = keep.tile([P, MB], F32, name="emph_sb")[:]
         wgo_sb = keep.tile([P, S], F32, name="wgo_sb")
         prior_sb = [keep.tile([P, S], F32, name=f"prior{m}") for m in range(MB)]
         weight = [raw["w2", 0, m // 2][:, (m % 2) * S:(m % 2 + 1) * S] for m in range(MB)]
@@ -83,13 +83,15 @@ def tile_list_netball_selection_page_kernel(
                 frac[b, jb] = keep.tile([P, PACK, P], F32, name=f"frac_{b}{jb}")
         hc = [keep.tile([P, S], U32, name=f"hc{b}", align_bytes=64) for b in range(PASSES)]
         hs = [keep.tile([P, S], U8, name=f"hs{b}", align_bytes=64) for b in range(PASSES)]
-        staging = [keep.tile([P, KP * PACK], BF16, name=f"staging{n}", align_bytes=64) for n in range(3)]
+        staging = [keep.tile([P, KP * PACK], BF16, name=f"staging{n}", align_bytes=64) for n in range(4)]
 
-        for plane in (w3s, tabs, tab2s, vs_low, w3sp[1]):
+        for plane in (w3s, tabs):
             nc.gpsimd.memset(plane[:].bitcast(I32), 0)
-        make_identity(nc, ident[:])
-        warm = keep.tile([P, 1], F32, name="warm")
-        nc.scalar.activation(warm[:], ident[:, 0:1], ACT.Silu)
+        for plane in (tab2s, vs_low, w3sp[1]):
+            nc.vector.memset(plane[:].bitcast(I32), 0)
+        warm = keep.tile([P, 2], F32, name="warm")
+        nc.vector.memset(warm[:, 0:1], 0.0)
+        nc.scalar.activation(warm[:, 1:2], warm[:, 0:1], ACT.Silu)
 
         def load_w_pass(name, n, a):
             c0, c1 = pieces[name][n]
@@ -105,22 +107,22 @@ def tile_list_netball_selection_page_kernel(
         def load_words(dst, src, a):
             nc.sync.dma_start(out=dst[a][:], in_=src[a].rearrange("p t i -> p (t i)").bitcast(I32))
 
-        def load_planes(dst, src):
+        def load_planes(dst, src, queue):
             for q in range(4):
-                nc.sync.dma_start(
+                queue.dma_start(
                     out=dst[32 * q:32 * q + 4 * PASSES, :].bitcast(I32),
                     in_=src[:, 4 * q:4 * q + 4, :].bitcast(I32),
                 )
 
         def lower_plane(dst, src):
-            nc.sync.dma_start(out=dst[0:P - 4, :].bitcast(I32), in_=src[4:P, :].bitcast(I32))
+            nc.gpsimd.dma_start(out=dst[0:P - 4, :].bitcast(I32), in_=src[4:P, :].bitcast(I32))
 
         grouped = {}
 
         def cast(name, n, a, engine, lo, hi):
             c0, c1 = pieces[name][n]
             if (name, n, a) not in grouped:
-                grouped[name, n, a] = staging[len(grouped) % 3][:, 0:(c1 - c0) * PACK]
+                grouped[name, n, a] = staging[len(grouped) % 4][:, 0:(c1 - c0) * PACK]
             d0, d1 = (c1 - c0) * lo // 8, (c1 - c0) * hi // 8
             dst = grouped[name, n, a][:, d0 * PACK:d1 * PACK].rearrange("p (c i j) -> p c j i", i=4, j=PACK)
             src = raw[name, n, a][:].rearrange("p (j c) -> p j c", j=PACK)[:, :, d0:d1].rearrange("p j (c i) -> p c j i", i=4)
@@ -177,10 +179,12 @@ def tile_list_netball_selection_page_kernel(
 
         forms = {}
 
-        def tanh(n, jb):
+        def tanh(n, jb, host=None, slot=0):
             x, b, ms = sums["w1", n, jb]
-            if (b, jb) not in forms:
-                forms[b, jb] = ring.tile([P, PACK, P], F32, name="form", bufs=3)
+            if host is None:
+                forms[b, jb] = ring.tile([P, PACK, P], F32, name="form", bufs=3)[:]
+            else:
+                forms[b, jb] = host[:, slot * KP:(slot + 1) * KP].rearrange("p (t j) -> p t j", t=PACK)
             nc.scalar.activation(forms[b, jb][:, :, ms], x, ACT.Tanh)
 
         looks = {}
@@ -206,13 +210,16 @@ def tile_list_netball_selection_page_kernel(
             both = banks[bank][:].rearrange("p (t j) -> p t j", t=PACK)
             boths[b, jb] = both
             for t in range(PACK):
-                nc.tensor.matmul(both[:, t, :], forms[b, jb][:, t, :], ident[:], start=True, stop=False, is_transpose=True)
-                nc.tensor.matmul(both[:, t, :], wave[b, jb][:, t, :], ident[:], start=False, stop=True, is_transpose=True)
+                nc.tensor.matmul(both[:, t, :], forms[b, jb][:, t, :], ident, start=True, stop=False, is_transpose=True)
+                nc.tensor.matmul(both[:, t, :], wave[b, jb][:, t, :], ident, start=False, stop=True, is_transpose=True)
 
         gained = {}
 
-        def apply_gain(b, jb):
-            gained[b, jb] = ring.tile([P, PACK, P], F32, name="gained", bufs=3)
+        def apply_gain(b, jb, host=None, slot=0):
+            if host is None:
+                gained[b, jb] = ring.tile([P, PACK, P], F32, name="gained", bufs=3)[:]
+            else:
+                gained[b, jb] = host[:, slot * KP:(slot + 1) * KP].rearrange("p (t j) -> p t j", t=PACK)
             for t in range(PACK):
                 nc.scalar.activation(gained[b, jb][:, t, :], boths[b, jb][:, t, :], ACT.Copy, scale=gain_sb[:, b, t:t + 1])
 
@@ -225,7 +232,7 @@ def tile_list_netball_selection_page_kernel(
             nc.vector.tensor_tensor(
                 hb[b, half][:, within * KP:(within + 1) * KP].rearrange("p (c i t) -> p c t i", i=4, t=PACK),
                 looks[b, jb].rearrange("p t (c i) -> p c t i", i=4),
-                gained[b, jb][:].rearrange("p t (c i) -> p c t i", i=4),
+                gained[b, jb].rearrange("p t (c i) -> p c t i", i=4),
                 ALU.max,
             )
 
@@ -250,15 +257,18 @@ def tile_list_netball_selection_page_kernel(
 
         score = {}
 
-        def add_prior(m, half):
+        def add_prior(m, half, host=None):
             cols = slice(half * HALF, (half + 1) * HALF)
-            score[m, half] = ring.tile([P, HALF], F32, name="score", bufs=3)
-            nc.vector.tensor_tensor(score[m, half][:], es[m, half], prior_sb[m][:, cols], ALU.add)
+            if host is None:
+                score[m, half] = ring.tile([P, HALF], F32, name="score", bufs=3)[:]
+            else:
+                score[m, half] = host.bitcast(F32)[:, 0:HALF]
+            nc.vector.tensor_tensor(score[m, half], es[m, half], prior_sb[m][:, cols], ALU.add)
 
         def place(m, half):
             cols = slice(half * HALF, (half + 1) * HALF)
             entries = slice(half * HALF // 16, (half + 1) * HALF // 16)
-            nc.vector.tensor_tensor(page[m][:].indirect(idx3[:, entries]), score[m, half][:], weight[m][:, cols], ALU.mult)
+            nc.vector.tensor_tensor(page[m][:].indirect(idx3[:, entries]), score[m, half], weight[m][:, cols], ALU.mult)
             if half == 1:
                 nc.sync.dma_start(out=out[m * P:(m + 1) * P, :], in_=page[m][:])
 
@@ -305,174 +315,152 @@ def tile_list_netball_selection_page_kernel(
         load_words(tabw, tab_words, 0)
         nc.sync.dma_start(idx[:], offs)
         nc.sync.dma_start(out=gain_sb[:], in_=gain.rearrange("(b p t) -> p b t", b=PASSES, t=PACK))
-        load_planes(w3s, w3_scales)
+        load_planes(w3s, w3_scales, nc.sync)
         load_words(tabw, tab_words, 1)
-        load_planes(tabs, tab_scales)
+        load_planes(tabs, tab_scales, nc.sync)
         load_w("w2", 0)
+        nc.sync.dma_start(idx2[:], offs2)
         load_w("w2", 1)
-
-        gather_words(vw[0], tabw[0], idx)
-        permute_w3_scales()
-        gather_words(vw[1], tabw[1], idx)
-        gather_bytes(vs, tabs, idx)
-        lower_plane(vs_low, vs)
         load_w("w1", 0)
         load_w_pass("w2", 2, 0)
         load_w3()
         load_w_pass("w2", 2, 1)
-        nc.sync.dma_start(idx2[:], offs2)
-        load_planes(tab2s, tab2_scales)
         load_w("w1", 1)
         load_w("w1", 2)
         load_words(tab2w, tab2_words, 0)
         load_words(tab2w, tab2_words, 1)
         nc.sync.dma_start(idx3[:], offs3)
         with nc.allow_non_contiguous_dma(reason="one emphasis value a row of the page"):
-            nc.sync.dma_start(out=emph_sb[:], in_=emph.rearrange("(m p) -> p m", p=P))
+            nc.sync.dma_start(out=emph_sb, in_=emph.rearrange("(m p) -> p m", p=P))
         load_page()
+
+        gather_words(vw[0], tabw[0], idx)
+        permute_w3_scales()
+        gather_words(vw[1], tabw[1], idx)
+        gather_bytes(vs, tabs, idx)
+        lower_plane(vs_low, vs)
+        load_planes(tab2s, tab2_scales, nc.gpsimd)
         cast("w2", 0, 0, "s", 0, 8)
         quant("w2", 0, 0)
         cast("w2", 0, 1, "s", 0, 3)
         cast("w2", 0, 1, "v", 3, 8)
         quant("w2", 0, 1)
-        for jb in range(JB):
-            product("w2", [0], jb, jb)
         cast("w2", 1, 0, "s", 0, 8)
-        cast("w2", 1, 1, "s", 0, 8)
         quant("w2", 1, 0)
-        count_turns(0, 0)
-        count_turns(0, 1)
+        make_identity(nc, ident)
+        cast("w2", 1, 1, "s", 0, 8)
         quant("w2", 1, 1)
-        for jb in range(JB):
-            product("w2", [1], jb, 4 + jb)
-        fraction(0, 0)
-        fraction(0, 1)
         cast("w1", 0, 0, "s", 0, 8)
-        count_turns(1, 0)
-        count_turns(1, 1)
-        fraction(1, 0)
-        fraction(1, 1)
-        count_turns(0, 2)
-        count_turns(0, 3)
         quant("w1", 0, 0)
         cast("w1", 0, 1, "s", 0, 8)
-        fraction(0, 2)
-        fraction(0, 3)
-        count_turns(1, 2)
-        count_turns(1, 3)
-        fraction(1, 2)
-        fraction(1, 3)
         quant("w1", 0, 1)
-        product("w1", [0], 0, 0)
-        product("w1", [0], 1, 1)
-        sine(0, 0, raw["w1", 0, 1], 0)
-        sine(0, 1, raw["w1", 0, 1], 1)
-        permute_w3_words(1)
-        permute_w3_words(0)
         cast("w2", 2, 0, "s", 0, 5)
         cast("w2", 2, 0, "v", 5, 8)
-        tanh(0, 0)
         quant("w2", 2, 0)
-        turn(0, 0, 2)
-        look_of(0, 0, 4)
         cast("w2", 2, 1, "s", 0, 5)
         cast("w2", 2, 1, "v", 5, 8)
-        tanh(0, 1)
-        gather_bytes(v2s, tab2s, idx2)
         quant("w2", 2, 1)
-        product("w2", [2], 0, 0)
-        turn(0, 1, 3)
-        product("w2", [2], 1, 1)
-        look_of(0, 1, 5)
-        look_of(1, 0, 6)
-        look_of(1, 1, 7)
         cast("w1", 1, 0, "s", 0, 8)
         quant("w1", 1, 0)
         cast("w1", 1, 1, "s", 0, 8)
-        apply_gain(0, 0)
-        count_turns(2, 0)
         quant("w1", 1, 1)
         cast("w1", 2, 0, "s", 0, 8)
-        fraction(2, 0)
         quant("w1", 2, 0)
         cast("w1", 2, 1, "s", 0, 3)
         cast("w1", 2, 1, "v", 3, 8)
-        count_turns(2, 1)
         quant("w1", 2, 1)
-        apply_gain(0, 1)
-        product("w1", [1, 2], 0, 2)
-        fraction(2, 1)
-        feature(0, 0)
-        sine(1, 0, raw["w2", 2, 1], 0)
-        product("w1", [1, 2], 1, 3)
-        product("w2", [2], 2, 0)
-        product("w2", [2], 3, 1)
+        for n in (0, 1):
+            for jb in range(JB):
+                product("w2", [n], jb, JB * n + jb)
+        for pair in ((0, 1), (2, 3)):
+            for n in (0, 1):
+                for jb in pair:
+                    count_turns(n, jb)
+                for jb in pair:
+                    fraction(n, jb)
+        for jb in (0, 1):
+            product("w1", [0], jb, jb)
+            sine(0, jb, raw["w1", 0, 1], jb)
+        permute_w3_words(1)
+        permute_w3_words(0)
+        tanh(0, 0, raw["w2", 2, 0], 0)
+        tanh(0, 1, raw["w2", 2, 1], 0)
+        for jb in (0, 1):
+            product("w2", [2], jb, jb)
+            product("w1", [1, 2], jb, 6 + jb)
+            turn(0, jb, 2 + jb)
+            look_of(0, jb, 4 + jb)
+        for jb in (0, 1):
+            count_turns(2, jb)
+            fraction(2, jb)
+        apply_gain(0, 0, raw["w1", 1, 1], 0)
+        apply_gain(0, 1, raw["w1", 2, 1], 0)
+        for jb in (0, 1):
+            feature(0, jb)
+        sine(1, 0, raw["w1", 2, 1], 1)
         tanh(1, 0)
-        feature(0, 1)
-        gather_words(v2w[0], tab2w[0], idx2)
-        sine(1, 1, raw["w2", 2, 1], 1)
+        sine(1, 1, raw["w1", 2, 0], 0)
         tanh(1, 1)
-        turn(1, 0, 4)
-        turn(1, 1, 5)
+        for jb in (0, 1):
+            turn(1, jb, 2 + jb)
+            look_of(1, jb, 4 + jb)
+            apply_gain(1, jb)
+            feature(1, jb)
         quant_h(0, 0)
-        count_turns(2, 2)
-        apply_gain(1, 0)
-        apply_gain(1, 1)
-        product("w1", [0], 2, 2)
-        product("w1", [0], 3, 3)
-        gather_words(v2w[1], tab2w[1], idx2)
-        feature(1, 0)
-        feature(1, 1)
-        fraction(2, 2)
         quant_h(1, 0)
-        count_turns(2, 3)
+        gather_bytes(v2s, tab2s, idx2)
+        for a in range(PASSES):
+            gather_words(v2w[a], tab2w[a], idx2)
         weigh(0, "s")
+        for jb in (2, 3):
+            product("w1", [0], jb, 4 + jb)
+        sine(0, 2, raw["w1", 1, 1], 0)
+        tanh(0, 2)
+        sine(0, 3, raw["w1", 2, 1], 0)
+        tanh(0, 3)
         meet(0, 0, 6)
         meet(1, 0, 7)
+        for jb in (2, 3):
+            product("w2", [2], jb, jb - 2)
+        count_turns(2, 2, staging[3][:])
+        fraction(2, 2)
+        count_turns(2, 3, hb[1, 0][:])
         fraction(2, 3)
-        sine(0, 2, raw["w1", 2, 1], 0)
-        tanh(0, 2)
-        sine(0, 3, raw["w1", 2, 1], 1)
-        tanh(0, 3)
-        turn(0, 2, 4)
-        look_of(0, 2, 0)
-        turn(0, 3, 5)
-        look_of(0, 3, 1)
-        product("w1", [1, 2], 2, 2)
-        product("w1", [1, 2], 3, 3)
+        for jb in (2, 3):
+            turn(0, jb, jb)
+            look_of(0, jb, jb + 2)
+            product("w1", [1, 2], jb, jb - 2)
         weigh(1, "s")
-        apply_gain(0, 2)
-        sine(1, 2, raw["w1", 2, 0], 0)
-        apply_gain(0, 3)
+        for jb in (2, 3):
+            apply_gain(0, jb)
         add_prior(0, 0)
         add_prior(1, 0)
         place(0, 0)
         meet(2, 0, 6)
         meet(3, 0, 7)
         weigh(2, "s")
+        sine(1, 2, raw["w2", 2, 0], 0)
         tanh(1, 2)
-        sine(1, 3, raw["w1", 2, 0], 1)
+        sine(1, 3, raw["w2", 2, 1], 0)
         tanh(1, 3)
         weigh(3, "s")
         place(1, 0)
-        feature(0, 2)
-        feature(0, 3)
-        turn(1, 2, 4)
-        look_of(1, 2, 0)
-        turn(1, 3, 5)
-        look_of(1, 3, 1)
+        for jb in (2, 3):
+            feature(0, jb)
+            turn(1, jb, jb)
+            look_of(1, jb, jb + 2)
         add_prior(2, 0)
         quant_h(0, 1)
-        apply_gain(1, 2)
-        apply_gain(1, 3)
+        for jb in (2, 3):
+            apply_gain(1, jb)
         place(2, 0)
-        add_prior(3, 0)
-        feature(1, 2)
-        feature(1, 3)
+        for jb in (2, 3):
+            feature(1, jb)
         quant_h(1, 1)
+        add_prior(3, 0, hb[1, 1][:])
         place(3, 0)
         for m in range(MB):
-            meet(m, 1, (6, 7, 2, 3)[m])
+            meet(m, 1, (6, 7, 0, 1)[m])
         add_prior(0, 1)
         for m in range(MB):
             if m + 1 < MB:

@@ -22,12 +22,22 @@ P = 128
 PACK = 4
 KP = P * PACK
 PASSES = K // KP
-JB = S // P
-MB = S2 // P
+BLOCKS = S // P
+PAGES = S2 // P
 HALF = S // 2
+FIRST, SECOND = (0, 1), (2, 3)
+LIST_ROW = 16
+QUADRANTS, QUADRANT = 4, 32
+ROWS = 4
+RUN = 4
 TWO_PI = 2.0 * math.pi
-W2_PIECES = [(0, 256), (256, 512), (512, 1024)]
-W1_PIECES = [(0, 512), (512, 768), (768, 1024)]
+MX_ALIGN = 64
+
+PIECES = {"w2": [(0, 256), (256, 512), (512, 1024)], "w1": [(0, 512), (512, 768), (768, 1024)]}
+EIGHTHS = 8
+SCALAR_SHARE = {("w2", 0, 1): 3, ("w1", 2, 1): 3, ("w2", 2, 0): 5, ("w2", 2, 1): 5}
+STAGING = 4
+DEPTH = 3
 
 
 def tile_list_netball_selection_page_kernel(
@@ -41,216 +51,218 @@ def tile_list_netball_selection_page_kernel(
         psum = ctx.enter_context(tc.psum_pool(name="psum", bufs=1))
         banks = [psum.tile([P, KP], F32, name=f"bank{n}") for n in range(8)]
 
-        idx = keep.tile([P, S // 16], U16, name="idx")
-        idx2 = keep.tile([P, S2 // 16], U16, name="idx2")
-        idx3 = keep.tile([P, S // 16], U16, name="idx3")
+        idx = keep.tile([P, S // LIST_ROW], U16, name="idx")
+        idx2 = keep.tile([P, S2 // LIST_ROW], U16, name="idx2")
+        idx3 = keep.tile([P, S // LIST_ROW], U16, name="idx3")
         gain_sb = keep.tile([P, PASSES, PACK], F32, name="gain_sb")
 
-        tabw = [keep.tile([P, T], I32, name=f"tabw{a}", align_bytes=64) for a in range(PASSES)]
-        tab2w = [keep.tile([P, T3], I32, name=f"tab2w{a}", align_bytes=64) for a in range(PASSES)]
-        tabs = keep.tile([P, T], U8, name="tabs", align_bytes=64)
-        tab2s = keep.tile([P, T3], U8, name="tab2s", align_bytes=64)
-        w3w = keep.tile([P, PASSES, 2 * H], U8, name="w3w", align_bytes=64)
-        w3s = keep.tile([P, H], U8, name="w3s", align_bytes=64)
-        w3wp = keep.tile([P, PASSES, 2 * H], U8, name="w3wp", align_bytes=64)
-        w3sp = [keep.tile([P, H], U8, name=f"w3sp{a}", align_bytes=64) for a in range(PASSES)]
-        vw = [keep.tile([P, S], U32, name=f"vw{a}", align_bytes=64) for a in range(PASSES)]
-        vs = keep.tile([P, S], U8, name="vs", align_bytes=64)
-        vs_low = keep.tile([P, S], U8, name="vs_low", align_bytes=64)
-        v2w = [keep.tile([P, S2], U32, name=f"v2w{a}", align_bytes=64) for a in range(PASSES)]
-        v2s = keep.tile([P, S2], U8, name="v2s", align_bytes=64)
+        tabw = [keep.tile([P, T], I32, name=f"tabw{a}", align_bytes=MX_ALIGN) for a in range(PASSES)]
+        tab2w = [keep.tile([P, T3], I32, name=f"tab2w{a}", align_bytes=MX_ALIGN) for a in range(PASSES)]
+        tabs = keep.tile([P, T], U8, name="tabs", align_bytes=MX_ALIGN)
+        tab2s = keep.tile([P, T3], U8, name="tab2s", align_bytes=MX_ALIGN)
+        w3w = keep.tile([P, PASSES, 2 * H], U8, name="w3w", align_bytes=MX_ALIGN)
+        w3s = keep.tile([P, H], U8, name="w3s", align_bytes=MX_ALIGN)
+        w3wp = keep.tile([P, PASSES, 2 * H], U8, name="w3wp", align_bytes=MX_ALIGN)
+        w3sp = [keep.tile([P, H], U8, name=f"w3sp{a}", align_bytes=MX_ALIGN) for a in range(PASSES)]
+        vw = [keep.tile([P, S], U32, name=f"vw{a}", align_bytes=MX_ALIGN) for a in range(PASSES)]
+        vs = keep.tile([P, S], U8, name="vs", align_bytes=MX_ALIGN)
+        vs_low = keep.tile([P, S], U8, name="vs_low", align_bytes=MX_ALIGN)
+        v2w = [keep.tile([P, S2], U32, name=f"v2w{a}", align_bytes=MX_ALIGN) for a in range(PASSES)]
+        v2s = keep.tile([P, S2], U8, name="v2s", align_bytes=MX_ALIGN)
         weights = {"w1": w1, "w2": w2}
-        pieces = {"w1": W1_PIECES, "w2": W2_PIECES}
         raw = {}
         codes = {}
         for name in ("w2", "w1"):
-            for n, (c0, c1) in enumerate(pieces[name]):
+            for n, (c0, c1) in enumerate(PIECES[name]):
                 for a in range(PASSES):
-                    raw[name, n, a] = keep.tile([P, PACK * (c1 - c0)], F32, name=f"raw_{name}{n}{a}", align_bytes=64)
-                    codes[name, n, a] = (
-                        keep.tile([P, c1 - c0], U32, name=f"wc_{name}{n}{a}", align_bytes=64),
-                        keep.tile([P, c1 - c0], U8, name=f"ws_{name}{n}{a}", align_bytes=64),
+                    raw[name, n, a] = keep.tile(
+                        [P, PACK * (c1 - c0)], F32, name=f"raw_{name}{n}{a}", align_bytes=MX_ALIGN
                     )
-        ident = keep.tile([P, P], F32, name="ident")[:]
-        emph_sb = keep.tile([P, MB], F32, name="emph_sb")[:]
+                    codes[name, n, a] = (
+                        keep.tile([P, c1 - c0], U32, name=f"wc_{name}{n}{a}", align_bytes=MX_ALIGN),
+                        keep.tile([P, c1 - c0], U8, name=f"ws_{name}{n}{a}", align_bytes=MX_ALIGN),
+                    )
+        ident = keep.tile([P, P], F32, name="ident")
+        emph_sb = keep.tile([P, PAGES], F32, name="emph_sb")
         wgo_sb = keep.tile([P, S], F32, name="wgo_sb")
-        prior_sb = [keep.tile([P, S], F32, name=f"prior{m}") for m in range(MB)]
-        weight = [raw["w2", 0, m // 2][:, (m % 2) * S:(m % 2 + 1) * S] for m in range(MB)]
-        page = [keep.tile([P, T2], F32, name=f"page{m}") for m in range(MB)]
+        prior_sb = [keep.tile([P, S], F32, name=f"prior{m}") for m in range(PAGES)]
+        page = [keep.tile([P, T2], F32, name=f"page{m}") for m in range(PAGES)]
         frac = {}
-        for b in range(PASSES):
-            for jb in range(JB):
-                frac[b, jb] = keep.tile([P, PACK, P], F32, name=f"frac_{b}{jb}")
-        hc = [keep.tile([P, S], U32, name=f"hc{b}", align_bytes=64) for b in range(PASSES)]
-        hs = [keep.tile([P, S], U8, name=f"hs{b}", align_bytes=64) for b in range(PASSES)]
-        staging = [keep.tile([P, KP * PACK], BF16, name=f"staging{n}", align_bytes=64) for n in range(4)]
+        for g in range(PASSES):
+            for c in range(BLOCKS):
+                frac[g, c] = keep.tile([P, PACK, P], F32, name=f"frac_{g}{c}")
+        hc = [keep.tile([P, S], U32, name=f"hc{g}", align_bytes=MX_ALIGN) for g in range(PASSES)]
+        hs = [keep.tile([P, S], U8, name=f"hs{g}", align_bytes=MX_ALIGN) for g in range(PASSES)]
+        staging = [keep.tile([P, KP * PACK], BF16, name=f"staging{n}", align_bytes=MX_ALIGN) for n in range(STAGING)]
 
-        for plane in (w3s, tabs):
-            nc.gpsimd.memset(plane[:].bitcast(I32), 0)
-        for plane in (tab2s, vs_low, w3sp[1]):
+        def spot(name, n, a, slot=0):
+            return raw[name, n, a][:, slot * KP:(slot + 1) * KP]
+
+        def quarters(ap):
+            return ap.rearrange("p (t m) -> p t m", t=PACK)
+
+        page_weight = [spot("w2", 0, m // 2, m % 2) for m in range(PAGES)]
+
+        nc.gpsimd.memset(tabs[:].bitcast(I32), 0)
+        for plane in (w3s, tab2s, vs_low, w3sp[1]):
             nc.vector.memset(plane[:].bitcast(I32), 0)
         warm = keep.tile([P, 2], F32, name="warm")
         nc.vector.memset(warm[:, 0:1], 0.0)
         nc.scalar.activation(warm[:, 1:2], warm[:, 0:1], ACT.Silu)
 
-        def load_w_pass(name, n, a):
-            c0, c1 = pieces[name][n]
-            src = weights[name][a * KP:(a + 1) * KP, c0:c1]
+        def load_pass(name, n, a):
+            c0, c1 = PIECES[name][n]
             nc.sync.dma_start(
-                out=raw[name, n, a][:].rearrange("p (j c) -> p j c", j=PACK), in_=src.rearrange("(p j) c -> p j c", j=PACK)
+                out=raw[name, n, a][:].rearrange("p (i c) -> p i c", i=PACK),
+                in_=weights[name][a * KP:(a + 1) * KP, c0:c1].rearrange("(p i) c -> p i c", i=PACK),
             )
 
-        def load_w(name, n):
+        def load_piece(name, n):
             for a in range(PASSES):
-                load_w_pass(name, n, a)
+                load_pass(name, n, a)
 
         def load_words(dst, src, a):
             nc.sync.dma_start(out=dst[a][:], in_=src[a].rearrange("p t i -> p (t i)").bitcast(I32))
 
-        def load_planes(dst, src, queue):
-            for q in range(4):
+        def load_plane(dst, src, queue):
+            for q in range(QUADRANTS):
                 queue.dma_start(
-                    out=dst[32 * q:32 * q + 4 * PASSES, :].bitcast(I32),
-                    in_=src[:, 4 * q:4 * q + 4, :].bitcast(I32),
+                    out=dst[QUADRANT * q:QUADRANT * q + ROWS * PASSES, :].bitcast(I32),
+                    in_=src[:, ROWS * q:ROWS * (q + 1), :].bitcast(I32),
                 )
 
         def lower_plane(dst, src):
-            nc.gpsimd.dma_start(out=dst[0:P - 4, :].bitcast(I32), in_=src[4:P, :].bitcast(I32))
+            nc.gpsimd.dma_start(out=dst[0:P - ROWS, :].bitcast(I32), in_=src[ROWS:P, :].bitcast(I32))
 
-        grouped = {}
+        def gather_words(dst, src, by):
+            nc.vector.tensor_copy(dst[:], src[:].bitcast(U32).indirect(by[:]))
 
-        def cast(name, n, a, engine, lo, hi):
-            c0, c1 = pieces[name][n]
-            if (name, n, a) not in grouped:
-                grouped[name, n, a] = staging[len(grouped) % 4][:, 0:(c1 - c0) * PACK]
-            d0, d1 = (c1 - c0) * lo // 8, (c1 - c0) * hi // 8
-            dst = grouped[name, n, a][:, d0 * PACK:d1 * PACK].rearrange("p (c i j) -> p c j i", i=4, j=PACK)
-            src = raw[name, n, a][:].rearrange("p (j c) -> p j c", j=PACK)[:, :, d0:d1].rearrange("p j (c i) -> p c j i", i=4)
-            if engine == "s":
-                nc.scalar.copy(out=dst, in_=src)
-            elif engine == "g":
-                nc.gpsimd.tensor_scalar(dst, src, 1.0, 0.0, ALU.mult, ALU.add)
-            else:
-                nc.vector.tensor_copy(out=dst, in_=src)
+        def gather_bytes(dst, src, by):
+            nc.vector.tensor_copy(dst[:], src[:].indirect(by[:]))
 
-        def quant(name, n, a):
-            wc, ws = codes[name, n, a]
-            nc.vector.quantize_mx(out=wc[:].bitcast(FP8X4), scales=ws[:], in_=grouped[name, n, a])
+        def quantize_pass(name, n, a, stage):
+            width = PIECES[name][n][1] - PIECES[name][n][0]
+            split = width * SCALAR_SHARE.get((name, n, a), EIGHTHS) // EIGHTHS
+            rows = raw[name, n, a][:].rearrange("p (i c x) -> p c i x", i=PACK, x=RUN)
+            grouped = stage[:, 0:width * PACK]
+            words_in = grouped.rearrange("p (c x i) -> p c i x", x=RUN, i=PACK)
+            nc.scalar.copy(out=words_in[:, 0:split // RUN], in_=rows[:, 0:split // RUN])
+            if split < width:
+                nc.vector.tensor_copy(out=words_in[:, split // RUN:width // RUN], in_=rows[:, split // RUN:width // RUN])
+            words, plane = codes[name, n, a]
+            nc.vector.quantize_mx(out=words[:].bitcast(FP8X4), scales=plane[:], in_=grouped)
 
         sums = {}
 
-        def product(name, ns, jb, bank):
-            x = banks[bank]
-            cols = slice(jb * P, (jb + 1) * P)
-            base = pieces[name][ns[0]][0]
+        def product(name, ns, c, bank):
+            cols = slice(c * P, (c + 1) * P)
+            base = PIECES[name][ns[0]][0]
             for n in ns:
-                c0, c1 = pieces[name][n]
+                c0, c1 = PIECES[name][n]
                 for a in range(PASSES):
-                    wc, ws = codes[name, n, a]
+                    words, plane = codes[name, n, a]
                     nc.tensor.matmul_mx(
-                        out=x[:, c0 - base:c1 - base], lhsT=vw[a][:, cols].bitcast(FP8X4), lhsT_scale=vs[4 * a:P, cols],
-                        rhs=wc[:].bitcast(FP8X4), rhs_scale=ws[:], start=(a == 0), stop=(a == PASSES - 1),
+                        out=banks[bank][:, c0 - base:c1 - base],
+                        lhsT=vw[a][:, cols].bitcast(FP8X4), lhsT_scale=vs[ROWS * a:P, cols],
+                        rhs=words[:].bitcast(FP8X4), rhs_scale=plane[:],
+                        start=(a == 0), stop=(a == PASSES - 1),
                     )
-            width = pieces[name][ns[-1]][1] - base
-            sums[name, ns[0], jb] = (
-                x[:, 0:width].rearrange("p (m t) -> p t m", t=PACK), base // KP,
-                slice((base % KP) // PACK, (base % KP + width) // PACK),
+            width = PIECES[name][ns[-1]][1] - base
+            g, first = divmod(base, KP)
+            sums[name, ns[0], c] = (
+                banks[bank][:, 0:width].rearrange("p (m t) -> p t m", t=PACK), g,
+                slice(first // PACK, (first + width) // PACK),
             )
 
         turns = {}
 
-        def count_turns(n, jb, host=None):
-            x, b, ms = sums["w2", n, jb]
+        def count_turns(n, c, host=None):
+            x, g, ms = sums["w2", n, c]
             if host is None:
-                turns[n, jb] = ring.tile([P, PACK, ms.stop - ms.start], I32, name="turns", bufs=3)[:]
+                turns[n, c] = ring.tile([P, PACK, ms.stop - ms.start], I32, name="turns", bufs=DEPTH)[:]
             else:
-                turns[n, jb] = host.bitcast(I32)[:, 0:PACK * (ms.stop - ms.start)].rearrange("p (t m) -> p t m", t=PACK)
-            nc.vector.tensor_scalar(turns[n, jb], x, 1.0 / TWO_PI, None, ALU.mult)
+                turns[n, c] = quarters(host.bitcast(I32)[:, 0:KP])
+            nc.vector.tensor_scalar(turns[n, c], x, 1.0 / TWO_PI, None, ALU.mult)
 
-        def fraction(n, jb):
-            x, b, ms = sums["w2", n, jb]
-            nc.vector.scalar_tensor_tensor(frac[b, jb][:, :, ms], x, 1.0 / TWO_PI, turns[n, jb], ALU.mult, ALU.subtract)
+        def fraction(n, c):
+            x, g, ms = sums["w2", n, c]
+            nc.vector.scalar_tensor_tensor(frac[g, c][:, :, ms], x, 1.0 / TWO_PI, turns[n, c], ALU.mult, ALU.subtract)
 
         wave = {}
 
-        def sine(b, jb, host, slot):
-            wave[b, jb] = host[:, slot * KP:(slot + 1) * KP].rearrange("p (t m) -> p t m", t=PACK)
-            nc.scalar.activation(wave[b, jb], frac[b, jb][:], ACT.Sin, scale=TWO_PI)
+        def sine(g, c, host):
+            wave[g, c] = quarters(host)
+            nc.scalar.activation(wave[g, c], frac[g, c][:], ACT.Sin, scale=TWO_PI)
 
-        forms = {}
+        form = {}
 
-        def tanh(n, jb, host=None, slot=0):
-            x, b, ms = sums["w1", n, jb]
-            if host is None:
-                forms[b, jb] = ring.tile([P, PACK, P], F32, name="form", bufs=3)[:]
-            else:
-                forms[b, jb] = host[:, slot * KP:(slot + 1) * KP].rearrange("p (t j) -> p t j", t=PACK)
-            nc.scalar.activation(forms[b, jb][:, :, ms], x, ACT.Tanh)
+        def tanh(g, c, host=None):
+            x = sums["w1", g, c][0]
+            form[g, c] = ring.tile([P, PACK, P], F32, name="form", bufs=DEPTH)[:] if host is None else quarters(host)
+            nc.scalar.activation(form[g, c], x, ACT.Tanh)
 
-        looks = {}
+        look = {}
 
-        def look_of(b, jb, bank):
-            look = banks[bank][:].rearrange("p (t j) -> p t j", t=PACK)
-            looks[b, jb] = look
-            cols = slice(jb * P, (jb + 1) * P)
-            planes = (vs, vs_low)
+        def w3_product(g, c, bank):
+            look[g, c] = quarters(banks[bank][:])
+            cols = slice(c * P, (c + 1) * P)
+            v_planes = (vs, vs_low)
             for t in range(PACK):
-                c0 = b * KP + t * P
-                for n, a in enumerate((1, 0)):
+                c0 = g * KP + t * P
+                for a in reversed(range(PASSES)):
                     nc.tensor.matmul_mx(
-                        out=look[:, t, :], lhsT=w3wp[:, a, 2 * c0:2 * (c0 + P)].bitcast(FP4X4),
-                        lhsT_scale=w3sp[a][:, c0:c0 + P],
-                        rhs=vw[a][:, cols].bitcast(FP8X4), rhs_scale=planes[a][:, cols],
-                        start=(n == 0), stop=(n == PASSES - 1),
+                        out=look[g, c][:, t, :],
+                        lhsT=w3wp[:, a, 2 * c0:2 * (c0 + P)].bitcast(FP4X4), lhsT_scale=w3sp[a][:, c0:c0 + P],
+                        rhs=vw[a][:, cols].bitcast(FP8X4), rhs_scale=v_planes[a][:, cols],
+                        start=(a == PASSES - 1), stop=(a == 0),
                     )
 
-        boths = {}
+        both = {}
 
-        def turn(b, jb, bank):
-            both = banks[bank][:].rearrange("p (t j) -> p t j", t=PACK)
-            boths[b, jb] = both
+        def transpose_sum(g, c, bank):
+            both[g, c] = quarters(banks[bank][:])
             for t in range(PACK):
-                nc.tensor.matmul(both[:, t, :], forms[b, jb][:, t, :], ident, start=True, stop=False, is_transpose=True)
-                nc.tensor.matmul(both[:, t, :], wave[b, jb][:, t, :], ident, start=False, stop=True, is_transpose=True)
+                nc.tensor.matmul(both[g, c][:, t, :], form[g, c][:, t, :], ident[:], start=True, stop=False, is_transpose=True)
+                nc.tensor.matmul(both[g, c][:, t, :], wave[g, c][:, t, :], ident[:], start=False, stop=True, is_transpose=True)
 
         gained = {}
 
-        def apply_gain(b, jb, host=None, slot=0):
-            if host is None:
-                gained[b, jb] = ring.tile([P, PACK, P], F32, name="gained", bufs=3)[:]
-            else:
-                gained[b, jb] = host[:, slot * KP:(slot + 1) * KP].rearrange("p (t j) -> p t j", t=PACK)
+        def apply_gain(g, c, host=None):
+            gained[g, c] = (
+                ring.tile([P, PACK, P], F32, name="gained", bufs=DEPTH)[:] if host is None else quarters(host)
+            )
             for t in range(PACK):
-                nc.scalar.activation(gained[b, jb][:, t, :], boths[b, jb][:, t, :], ACT.Copy, scale=gain_sb[:, b, t:t + 1])
+                nc.scalar.activation(gained[g, c][:, t, :], both[g, c][:, t, :], ACT.Copy, scale=gain_sb[:, g, t:t + 1])
 
         hb = {}
 
-        def feature(b, jb):
-            half, within = divmod(jb, 2)
+        def feature(g, c):
+            half, within = divmod(c, 2)
             if within == 0:
-                hb[b, half] = ring.tile([P, HALF * PACK], BF16, name="hb", align_bytes=64)
+                hb[g, half] = ring.tile([P, HALF * PACK], BF16, name="hb", align_bytes=MX_ALIGN)
             nc.vector.tensor_tensor(
-                hb[b, half][:, within * KP:(within + 1) * KP].rearrange("p (c i t) -> p c t i", i=4, t=PACK),
-                looks[b, jb].rearrange("p t (c i) -> p c t i", i=4),
-                gained[b, jb].rearrange("p t (c i) -> p c t i", i=4),
+                hb[g, half][:, within * KP:(within + 1) * KP].rearrange("p (c x t) -> p c t x", x=RUN, t=PACK),
+                look[g, c].rearrange("p t (c x) -> p c t x", x=RUN),
+                gained[g, c].rearrange("p t (c x) -> p c t x", x=RUN),
                 ALU.max,
             )
 
-        def quant_h(b, half):
+        def quantize_h(g, half):
             cols = slice(half * HALF, (half + 1) * HALF)
-            nc.vector.quantize_mx(out=hc[b][:, cols].bitcast(FP8X4), scales=hs[b][:, cols], in_=hb[b, half][:])
+            nc.vector.quantize_mx(out=hc[g][:, cols].bitcast(FP8X4), scales=hs[g][:, cols], in_=hb[g, half][:])
 
-        es = {}
+        energy = {}
 
-        def meet(m, half, bank):
+        def second_product(m, half, bank):
             rows = slice(m * P, (m + 1) * P)
             cols = slice(half * HALF, (half + 1) * HALF)
-            e = banks[bank][:, 0:HALF]
-            es[m, half] = e
-            movers = [(a, vw[a], vs[4 * a:P, cols]) for a in range(PASSES)] + [(b, hc[b], hs[b][:, cols]) for b in range(PASSES)]
+            energy[m, half] = banks[bank][:, 0:HALF]
+            movers = [(a, vw[a], vs[ROWS * a:P, cols]) for a in range(PASSES)]
+            movers = movers + [(g, hc[g], hs[g][:, cols]) for g in range(PASSES)]
             for n, (a, words, plane) in enumerate(movers):
                 nc.tensor.matmul_mx(
-                    out=e, lhsT=v2w[a][:, rows].bitcast(FP8X4), lhsT_scale=v2s[4 * a:P, rows],
+                    out=energy[m, half],
+                    lhsT=v2w[a][:, rows].bitcast(FP8X4), lhsT_scale=v2s[ROWS * a:P, rows],
                     rhs=words[:, cols].bitcast(FP8X4), rhs_scale=plane,
                     start=(n == 0), stop=(n == len(movers) - 1),
                 )
@@ -260,209 +272,162 @@ def tile_list_netball_selection_page_kernel(
         def add_prior(m, half, host=None):
             cols = slice(half * HALF, (half + 1) * HALF)
             if host is None:
-                score[m, half] = ring.tile([P, HALF], F32, name="score", bufs=3)[:]
+                score[m, half] = ring.tile([P, HALF], F32, name="score", bufs=DEPTH)[:]
             else:
                 score[m, half] = host.bitcast(F32)[:, 0:HALF]
-            nc.vector.tensor_tensor(score[m, half], es[m, half], prior_sb[m][:, cols], ALU.add)
+            nc.vector.tensor_tensor(score[m, half], energy[m, half], prior_sb[m][:, cols], ALU.add)
+
+        def weigh(m):
+            nc.scalar.activation(page_weight[m], wgo_sb[:], ACT.Copy, scale=emph_sb[:, m:m + 1])
 
         def place(m, half):
             cols = slice(half * HALF, (half + 1) * HALF)
-            entries = slice(half * HALF // 16, (half + 1) * HALF // 16)
-            nc.vector.tensor_tensor(page[m][:].indirect(idx3[:, entries]), score[m, half], weight[m][:, cols], ALU.mult)
-            if half == 1:
-                nc.sync.dma_start(out=out[m * P:(m + 1) * P, :], in_=page[m][:])
-
-        def weigh(m, engine):
-            if engine == "g":
-                nc.gpsimd.tensor_scalar(weight[m], wgo_sb[:], emph_sb[:, m:m + 1], 0.0, ALU.mult, ALU.add)
-            else:
-                nc.scalar.activation(weight[m], wgo_sb[:], ACT.Copy, scale=emph_sb[:, m:m + 1])
-
-        def permute_w3_words(a):
-            nc.vector.tensor_copy(
-                out=w3wp[:, a, :].bitcast(U16).rearrange("p (b t m) -> p b t m", b=PASSES, t=PACK),
-                in_=w3w[:, a, :].bitcast(U16).rearrange("p (b m t) -> p b t m", b=PASSES, t=PACK),
+            entries = slice(half * HALF // LIST_ROW, (half + 1) * HALF // LIST_ROW)
+            nc.vector.tensor_tensor(
+                page[m][:].indirect(idx3[:, entries]), score[m, half], page_weight[m][:, cols], ALU.mult
             )
-
-        def permute_w3_scales():
-            nc.vector.tensor_copy(
-                out=w3sp[0][:].rearrange("p (b t m) -> p b t m", b=PASSES, t=PACK),
-                in_=w3s[:].rearrange("p (b m t) -> p b t m", b=PASSES, t=PACK),
-            )
-            lower_plane(w3sp[1], w3sp[0])
-
-        def gather_words(dst, src, by):
-            nc.vector.tensor_copy(dst[:], src[:].bitcast(U32).indirect(by[:]))
-
-        def gather_bytes(dst, src, by):
-            nc.vector.tensor_copy(dst[:], src[:].indirect(by[:]))
-
-        def load_small():
-            nc.sync.dma_start(idx[:], offs)
-            nc.sync.dma_start(out=gain_sb[:], in_=gain.rearrange("(b p t) -> p b t", b=PASSES, t=PACK))
-            with nc.allow_non_contiguous_dma(reason="one emphasis value a row of the page"):
-                nc.sync.dma_start(out=emph_sb[:], in_=emph.rearrange("(m p) -> p m", p=P))
-
-        def load_w3():
-            nc.sync.dma_start(out=w3w[:].bitcast(I32), in_=w3_words.rearrange("a p c -> p a c").bitcast(I32))
-
-        def load_page():
-            nc.sync.dma_start(out=wgo_sb[:], in_=wgo)
-            for m in range(MB):
-                nc.sync.dma_start(out=prior_sb[m][:], in_=prior[m * P:(m + 1) * P, :])
-                nc.sync.dma_start(out=page[m][:], in_=page1[m * P:(m + 1) * P, :])
 
         load_words(tabw, tab_words, 0)
         nc.sync.dma_start(idx[:], offs)
-        nc.sync.dma_start(out=gain_sb[:], in_=gain.rearrange("(b p t) -> p b t", b=PASSES, t=PACK))
-        load_planes(w3s, w3_scales, nc.sync)
+        load_plane(w3s, w3_scales, nc.sync)
         load_words(tabw, tab_words, 1)
-        load_planes(tabs, tab_scales, nc.sync)
-        load_w("w2", 0)
+        load_plane(tabs, tab_scales, nc.gpsimd)
+        load_piece("w2", 0)
         nc.sync.dma_start(idx2[:], offs2)
-        load_w("w2", 1)
-        load_w("w1", 0)
-        load_w_pass("w2", 2, 0)
-        load_w3()
-        load_w_pass("w2", 2, 1)
-        load_w("w1", 1)
-        load_w("w1", 2)
-        load_words(tab2w, tab2_words, 0)
-        load_words(tab2w, tab2_words, 1)
+        load_piece("w2", 1)
+        load_piece("w1", 0)
+        load_pass("w2", 2, 0)
+        nc.sync.dma_start(out=w3w[:].bitcast(I32), in_=w3_words.rearrange("a p c -> p a c").bitcast(I32))
+        load_pass("w2", 2, 1)
+        load_piece("w1", 1)
+        load_piece("w1", 2)
+        nc.sync.dma_start(out=gain_sb[:], in_=gain.rearrange("(g p t) -> p g t", g=PASSES, t=PACK))
+        for a in range(PASSES):
+            load_words(tab2w, tab2_words, a)
         nc.sync.dma_start(idx3[:], offs3)
-        with nc.allow_non_contiguous_dma(reason="one emphasis value a row of the page"):
-            nc.sync.dma_start(out=emph_sb, in_=emph.rearrange("(m p) -> p m", p=P))
-        load_page()
+        with nc.allow_non_contiguous_dma(reason="one emphasis value for each row of the page"):
+            nc.sync.dma_start(out=emph_sb[:], in_=emph.rearrange("(m p) -> p m", p=P))
+        nc.sync.dma_start(out=wgo_sb[:], in_=wgo)
+        for m in range(PAGES):
+            nc.sync.dma_start(out=prior_sb[m][:], in_=prior[m * P:(m + 1) * P, :])
+            nc.sync.dma_start(out=page[m][:], in_=page1[m * P:(m + 1) * P, :])
 
         gather_words(vw[0], tabw[0], idx)
-        permute_w3_scales()
+        nc.vector.tensor_copy(
+            out=w3sp[0][:].rearrange("p (g t m) -> p g t m", g=PASSES, t=PACK),
+            in_=w3s[:].rearrange("p (g m t) -> p g t m", g=PASSES, t=PACK),
+        )
+        lower_plane(w3sp[1], w3sp[0])
         gather_words(vw[1], tabw[1], idx)
         gather_bytes(vs, tabs, idx)
         lower_plane(vs_low, vs)
-        load_planes(tab2s, tab2_scales, nc.gpsimd)
-        cast("w2", 0, 0, "s", 0, 8)
-        quant("w2", 0, 0)
-        cast("w2", 0, 1, "s", 0, 3)
-        cast("w2", 0, 1, "v", 3, 8)
-        quant("w2", 0, 1)
-        cast("w2", 1, 0, "s", 0, 8)
-        quant("w2", 1, 0)
-        make_identity(nc, ident)
-        cast("w2", 1, 1, "s", 0, 8)
-        quant("w2", 1, 1)
-        cast("w1", 0, 0, "s", 0, 8)
-        quant("w1", 0, 0)
-        cast("w1", 0, 1, "s", 0, 8)
-        quant("w1", 0, 1)
-        cast("w2", 2, 0, "s", 0, 5)
-        cast("w2", 2, 0, "v", 5, 8)
-        quant("w2", 2, 0)
-        cast("w2", 2, 1, "s", 0, 5)
-        cast("w2", 2, 1, "v", 5, 8)
-        quant("w2", 2, 1)
-        cast("w1", 1, 0, "s", 0, 8)
-        quant("w1", 1, 0)
-        cast("w1", 1, 1, "s", 0, 8)
-        quant("w1", 1, 1)
-        cast("w1", 2, 0, "s", 0, 8)
-        quant("w1", 2, 0)
-        cast("w1", 2, 1, "s", 0, 3)
-        cast("w1", 2, 1, "v", 3, 8)
-        quant("w1", 2, 1)
+        load_plane(tab2s, tab2_scales, nc.gpsimd)
+        nc.vector.memset(ident[:], 0.0)
+        make_identity(nc, ident[:], nomemset=True)
+
+        stream = [("w2", 0), ("w2", 1), ("w1", 0), ("w2", 2), ("w1", 1), ("w1", 2)]
+        for step, (name, n) in enumerate(stream):
+            for a in range(PASSES):
+                quantize_pass(name, n, a, staging[(PASSES * step + a) % STAGING])
+        last_stage = staging[(PASSES * len(stream) - 1) % STAGING]
+
         for n in (0, 1):
-            for jb in range(JB):
-                product("w2", [n], jb, JB * n + jb)
-        for pair in ((0, 1), (2, 3)):
-            for n in (0, 1):
-                for jb in pair:
-                    count_turns(n, jb)
-                for jb in pair:
-                    fraction(n, jb)
-        for jb in (0, 1):
-            product("w1", [0], jb, jb)
-            sine(0, jb, raw["w1", 0, 1], jb)
-        permute_w3_words(1)
-        permute_w3_words(0)
-        tanh(0, 0, raw["w2", 2, 0], 0)
-        tanh(0, 1, raw["w2", 2, 1], 0)
-        for jb in (0, 1):
-            product("w2", [2], jb, jb)
-            product("w1", [1, 2], jb, 6 + jb)
-            turn(0, jb, 2 + jb)
-            look_of(0, jb, 4 + jb)
-        for jb in (0, 1):
-            count_turns(2, jb)
-            fraction(2, jb)
-        apply_gain(0, 0, raw["w1", 1, 1], 0)
-        apply_gain(0, 1, raw["w1", 2, 1], 0)
-        for jb in (0, 1):
-            feature(0, jb)
-        sine(1, 0, raw["w1", 2, 1], 1)
-        tanh(1, 0)
-        sine(1, 1, raw["w1", 2, 0], 0)
-        tanh(1, 1)
-        for jb in (0, 1):
-            turn(1, jb, 2 + jb)
-            look_of(1, jb, 4 + jb)
-            apply_gain(1, jb)
-            feature(1, jb)
-        quant_h(0, 0)
-        quant_h(1, 0)
+            for c in range(BLOCKS):
+                product("w2", [n], c, BLOCKS * n + c)
+        for n in (0, 1):
+            for pair in (FIRST, SECOND):
+                for c in pair:
+                    count_turns(n, c)
+                for c in pair:
+                    fraction(n, c)
+
+        for c in FIRST:
+            product("w1", [0], c, c)
+            sine(0, c, spot("w1", 0, 1, c))
+        for a in reversed(range(PASSES)):
+            nc.vector.tensor_copy(
+                out=w3wp[:, a, :].bitcast(U16).rearrange("p (g t m) -> p g t m", g=PASSES, t=PACK),
+                in_=w3w[:, a, :].bitcast(U16).rearrange("p (g m t) -> p g t m", g=PASSES, t=PACK),
+            )
+        for c in FIRST:
+            tanh(0, c, spot("w2", 2, c))
+        for c in FIRST:
+            product("w2", [2], c, c)
+            product("w1", [1, 2], c, 6 + c)
+            transpose_sum(0, c, 2 + c)
+            w3_product(0, c, 4 + c)
+        for c in FIRST:
+            count_turns(2, c)
+            fraction(2, c)
+        for c in FIRST:
+            apply_gain(0, c, spot("w1", 1 + c, 1))
+        for c in FIRST:
+            feature(0, c)
+        for c in FIRST:
+            sine(1, c, spot("w1", 2, 1 - c, 1 - c))
+            tanh(1, c)
+        for c in FIRST:
+            transpose_sum(1, c, 2 + c)
+            w3_product(1, c, 4 + c)
+            apply_gain(1, c)
+            feature(1, c)
+        for g in range(PASSES):
+            quantize_h(g, 0)
         gather_bytes(v2s, tab2s, idx2)
         for a in range(PASSES):
             gather_words(v2w[a], tab2w[a], idx2)
-        weigh(0, "s")
-        for jb in (2, 3):
-            product("w1", [0], jb, 4 + jb)
-        sine(0, 2, raw["w1", 1, 1], 0)
-        tanh(0, 2)
-        sine(0, 3, raw["w1", 2, 1], 0)
-        tanh(0, 3)
-        meet(0, 0, 6)
-        meet(1, 0, 7)
-        for jb in (2, 3):
-            product("w2", [2], jb, jb - 2)
-        count_turns(2, 2, staging[3][:])
-        fraction(2, 2)
-        count_turns(2, 3, hb[1, 0][:])
-        fraction(2, 3)
-        for jb in (2, 3):
-            turn(0, jb, jb)
-            look_of(0, jb, jb + 2)
-            product("w1", [1, 2], jb, jb - 2)
-        weigh(1, "s")
-        for jb in (2, 3):
-            apply_gain(0, jb)
-        add_prior(0, 0)
-        add_prior(1, 0)
+
+        weigh(0)
+        for c in SECOND:
+            product("w1", [0], c, 4 + c)
+        for c in SECOND:
+            sine(0, c, spot("w1", c - 1, 1))
+            tanh(0, c)
+        for m in (0, 1):
+            second_product(m, 0, 6 + m)
+        for c in SECOND:
+            product("w2", [2], c, c - 2)
+        for c, host in zip(SECOND, (last_stage, hb[1, 0])):
+            count_turns(2, c, host[:])
+            fraction(2, c)
+        for c in SECOND:
+            transpose_sum(0, c, c)
+            w3_product(0, c, 2 + c)
+            product("w1", [1, 2], c, c - 2)
+        weigh(1)
+        for c in SECOND:
+            apply_gain(0, c)
+        for m in (0, 1):
+            add_prior(m, 0)
         place(0, 0)
-        meet(2, 0, 6)
-        meet(3, 0, 7)
-        weigh(2, "s")
-        sine(1, 2, raw["w2", 2, 0], 0)
-        tanh(1, 2)
-        sine(1, 3, raw["w2", 2, 1], 0)
-        tanh(1, 3)
-        weigh(3, "s")
+        for m in (2, 3):
+            second_product(m, 0, 4 + m)
+        weigh(2)
+        for c in SECOND:
+            sine(1, c, spot("w2", 2, c - 2))
+            tanh(1, c)
+        weigh(3)
         place(1, 0)
-        for jb in (2, 3):
-            feature(0, jb)
-            turn(1, jb, jb)
-            look_of(1, jb, jb + 2)
+        for c in SECOND:
+            feature(0, c)
+            transpose_sum(1, c, c)
+            w3_product(1, c, 2 + c)
         add_prior(2, 0)
-        quant_h(0, 1)
-        for jb in (2, 3):
-            apply_gain(1, jb)
+        quantize_h(0, 1)
+        for c in SECOND:
+            apply_gain(1, c)
         place(2, 0)
-        for jb in (2, 3):
-            feature(1, jb)
-        quant_h(1, 1)
-        add_prior(3, 0, hb[1, 1][:])
-        place(3, 0)
-        for m in range(MB):
-            meet(m, 1, (6, 7, 0, 1)[m])
+        for c in SECOND:
+            feature(1, c)
+        quantize_h(1, 1)
+        add_prior(PAGES - 1, 0, hb[1, 1][:])
+        place(PAGES - 1, 0)
+
+        for m, bank in enumerate((6, 7, 0, 1)):
+            second_product(m, 1, bank)
         add_prior(0, 1)
-        for m in range(MB):
-            if m + 1 < MB:
+        for m in range(PAGES):
+            if m + 1 < PAGES:
                 add_prior(m + 1, 1)
             place(m, 1)
+            nc.sync.dma_start(out=out[m * P:(m + 1) * P, :], in_=page[m][:])

@@ -61,11 +61,11 @@ def tile_list_netball_selection_page_kernel(
         tabs = keep.tile([P, T], U8, name="tabs", align_bytes=MX_ALIGN)
         tab2s = keep.tile([P, T3], U8, name="tab2s", align_bytes=MX_ALIGN)
         w3w = keep.tile([P, PASSES, 2 * H], U8, name="w3w", align_bytes=MX_ALIGN)
-        w3s = keep.tile([P, H], U8, name="w3s", align_bytes=MX_ALIGN)
+        w3s = keep.tile([P, H], U8, name="w3s", tag="w3s", align_bytes=MX_ALIGN)
         w3wp = keep.tile([P, PASSES, 2 * H], U8, name="w3wp", align_bytes=MX_ALIGN)
         w3sp = [keep.tile([P, H], U8, name=f"w3sp{a}", align_bytes=MX_ALIGN) for a in range(PASSES)]
         vw = [keep.tile([P, S], U32, name=f"vw{a}", align_bytes=MX_ALIGN) for a in range(PASSES)]
-        vs = keep.tile([P, S], U8, name="vs", align_bytes=MX_ALIGN)
+        vs = keep.tile([P, S], U8, name="vs", tag="w3s", align_bytes=MX_ALIGN)
         vs_low = keep.tile([P, S], U8, name="vs_low", align_bytes=MX_ALIGN)
         v2w = [keep.tile([P, S2], U32, name=f"v2w{a}", align_bytes=MX_ALIGN) for a in range(PASSES)]
         v2s = keep.tile([P, S2], U8, name="v2s", align_bytes=MX_ALIGN)
@@ -293,8 +293,8 @@ def tile_list_netball_selection_page_kernel(
         load_words(tabw, tab_words, 1)
         load_plane(tabs, tab_scales, nc.gpsimd)
         load_piece("w2", 0)
-        nc.sync.dma_start(idx2[:], offs2)
         load_piece("w2", 1)
+        nc.sync.dma_start(idx2[:], offs2)
         load_piece("w1", 0)
         load_pass("w2", 2, 0)
         nc.sync.dma_start(out=w3w[:].bitcast(I32), in_=w3_words.rearrange("a p c -> p a c").bitcast(I32))

import math
from contextlib import ExitStack

import concourse.mybir as mybir
from concourse.masks import make_identity

K, T, S, H, T3, S2, T2 = 1024, 2048, 512, 1024, 2048, 512, 1024
FLOPS = 2 * (3 * K * H * S + 2 * H * S2 * S)

F32 = mybir.dt.float32
BF16 = mybir.dt.bfloat16
I32 = mybir.dt.int32
U32 = mybir.dt.uint32
U16 = mybir.dt.uint16
U8 = mybir.dt.uint8
FP8X4 = mybir.dt.float8_e4m3fn_x4
FP4X4 = mybir.dt.float4_e2m1fn_x4
ALU = mybir.AluOpType
ACT = mybir.ActivationFunctionType

P = 128
PACK = 4
KP = P * PACK
PASSES = K // KP
BLOCKS = S // P
PAGES = S2 // P
HALF = S // 2
FIRST, SECOND = (0, 1), (2, 3)
LIST_ROW = 16
QUADRANTS, QUADRANT = 4, 32
ROWS = 4
RUN = 4
TWO_PI = 2.0 * math.pi
MX_ALIGN = 64

PIECES = {"w2": [(0, 256), (256, 512), (512, 1024)], "w1": [(0, 512), (512, 768), (768, 1024)]}
EIGHTHS = 8
SCALAR_SHARE = {("w2", 0, 1): 3, ("w1", 2, 1): 3, ("w2", 2, 0): 5, ("w2", 2, 1): 5}
STAGING = 4
DEPTH = 3


def tile_list_netball_selection_page_kernel(
    tc, tab_words, tab_scales, offs, w1, w2, w3_words, w3_scales, gain, tab2_words, tab2_scales,
    offs2, prior, emph, offs3, wgo, page1, out,
):
    nc = tc.nc
    with ExitStack() as ctx:
        keep = ctx.enter_context(tc.tile_pool(name="keep", bufs=1))
        ring = ctx.enter_context(tc.tile_pool(name="ring", bufs=2))
        psum = ctx.enter_context(tc.psum_pool(name="psum", bufs=1))
        banks = [psum.tile([P, KP], F32, name=f"bank{n}") for n in range(8)]

        idx = keep.tile([P, S // LIST_ROW], U16, name="idx")
        idx2 = keep.tile([P, S2 // LIST_ROW], U16, name="idx2")
        idx3 = keep.tile([P, S // LIST_ROW], U16, name="idx3")
        gain_sb = keep.tile([P, PASSES, PACK], F32, name="gain_sb")

        tabw = [keep.tile([P, T], I32, name=f"tabw{a}", align_bytes=MX_ALIGN) for a in range(PASSES)]
        tab2w = [keep.tile([P, T3], I32, name=f"tab2w{a}", align_bytes=MX_ALIGN) for a in range(PASSES)]
        tabs = keep.tile([P, T], U8, name="tabs", align_bytes=MX_ALIGN)
        tab2s = keep.tile([P, T3], U8, name="tab2s", align_bytes=MX_ALIGN)
        w3w = keep.tile([P, PASSES, 2 * H], U8, name="w3w", align_bytes=MX_ALIGN)
        w3s = keep.tile([P, H], U8, name="w3s", tag="w3s", align_bytes=MX_ALIGN)
        w3wp = keep.tile([P, PASSES, 2 * H], U8, name="w3wp", align_bytes=MX_ALIGN)
        w3sp = [keep.tile([P, H], U8, name=f"w3sp{a}", align_bytes=MX_ALIGN) for a in range(PASSES)]
        vw = [keep.tile([P, S], U32, name=f"vw{a}", align_bytes=MX_ALIGN) for a in range(PASSES)]
        vs = keep.tile([P, S], U8, name="vs", tag="w3s", align_bytes=MX_ALIGN)
        vs_low = keep.tile([P, S], U8, name="vs_low", align_bytes=MX_ALIGN)
        v2w = [keep.tile([P, S2], U32, name=f"v2w{a}", align_bytes=MX_ALIGN) for a in range(PASSES)]
        v2s = keep.tile([P, S2], U8, name="v2s", align_bytes=MX_ALIGN)
        weights = {"w1": w1, "w2": w2}
        raw = {}
        codes = {}
        for name in ("w2", "w1"):
            for n, (c0, c1) in enumerate(PIECES[name]):
                for a in range(PASSES):
                    raw[name, n, a] = keep.tile(
                        [P, PACK * (c1 - c0)], F32, name=f"raw_{name}{n}{a}", align_bytes=MX_ALIGN
                    )
                    codes[name, n, a] = (
                        keep.tile([P, c1 - c0], U32, name=f"wc_{name}{n}{a}", align_bytes=MX_ALIGN),
                        keep.tile([P, c1 - c0], U8, name=f"ws_{name}{n}{a}", align_bytes=MX_ALIGN),
                    )
        ident = keep.tile([P, P], F32, name="ident")
        emph_sb = keep.tile([P, PAGES], F32, name="emph_sb")
        wgo_sb = keep.tile([P, S], F32, name="wgo_sb")
        prior_sb = [keep.tile([P, S], F32, name=f"prior{m}") for m in range(PAGES)]
        page = [keep.tile([P, T2], F32, name=f"page{m}") for m in range(PAGES)]
        frac = {}
        for g in range(PASSES):
            for c in range(BLOCKS):
                frac[g, c] = keep.tile([P, PACK, P], F32, name=f"frac_{g}{c}")
        hc = [keep.tile([P, S], U32, name=f"hc{g}", align_bytes=MX_ALIGN) for g in range(PASSES)]
        hs = [keep.tile([P, S], U8, name=f"hs{g}", align_bytes=MX_ALIGN) for g in range(PASSES)]
        staging = [keep.tile([P, KP * PACK], BF16, name=f"staging{n}", align_bytes=MX_ALIGN) for n in range(STAGING)]

        def spot(name, n, a, slot=0):
            return raw[name, n, a][:, slot * KP:(slot + 1) * KP]

        def quarters(ap):
            return ap.rearrange("p (t m) -> p t m", t=PACK)

        page_weight = [spot("w2", 0, m // 2, m % 2) for m in range(PAGES)]

        nc.gpsimd.memset(tabs[:].bitcast(I32), 0)
        for plane in (w3s, tab2s, vs_low, w3sp[1]):
            nc.vector.memset(plane[:].bitcast(I32), 0)
        warm = keep.tile([P, 2], F32, name="warm")
        nc.vector.memset(warm[:, 0:1], 0.0)
        nc.scalar.activation(warm[:, 1:2], warm[:, 0:1], ACT.Silu)

        def load_pass(name, n, a):
            c0, c1 = PIECES[name][n]
            nc.sync.dma_start(
                out=raw[name, n, a][:].rearrange("p (i c) -> p i c", i=PACK),
                in_=weights[name][a * KP:(a + 1) * KP, c0:c1].rearrange("(p i) c -> p i c", i=PACK),
            )

        def load_piece(name, n):
            for a in range(PASSES):
                load_pass(name, n, a)

        def load_words(dst, src, a):
            nc.sync.dma_start(out=dst[a][:], in_=src[a].rearrange("p t i -> p (t i)").bitcast(I32))

        def load_plane(dst, src, queue):
            for q in range(QUADRANTS):
                queue.dma_start(
                    out=dst[QUADRANT * q:QUADRANT * q + ROWS * PASSES, :].bitcast(I32),
                    in_=src[:, ROWS * q:ROWS * (q + 1), :].bitcast(I32),
                )

        def lower_plane(dst, src):
            nc.gpsimd.dma_start(out=dst[0:P - ROWS, :].bitcast(I32), in_=src[ROWS:P, :].bitcast(I32))

        def gather_words(dst, src, by):
            nc.vector.tensor_copy(dst[:], src[:].bitcast(U32).indirect(by[:]))

        def gather_bytes(dst, src, by):
            nc.vector.tensor_copy(dst[:], src[:].indirect(by[:]))

        def quantize_pass(name, n, a, stage):
            width = PIECES[name][n][1] - PIECES[name][n][0]
            split = width * SCALAR_SHARE.get((name, n, a), EIGHTHS) // EIGHTHS
            rows = raw[name, n, a][:].rearrange("p (i c x) -> p c i x", i=PACK, x=RUN)
            grouped = stage[:, 0:width * PACK]
            words_in = grouped.rearrange("p (c x i) -> p c i x", x=RUN, i=PACK)
            nc.scalar.copy(out=words_in[:, 0:split // RUN], in_=rows[:, 0:split // RUN])
            if split < width:
                nc.vector.tensor_copy(out=words_in[:, split // RUN:width // RUN], in_=rows[:, split // RUN:width // RUN])
            words, plane = codes[name, n, a]
            nc.vector.quantize_mx(out=words[:].bitcast(FP8X4), scales=plane[:], in_=grouped)

        sums = {}

        def product(name, ns, c, bank):
            cols = slice(c * P, (c + 1) * P)
            base = PIECES[name][ns[0]][0]
            for n in ns:
                c0, c1 = PIECES[name][n]
                for a in range(PASSES):
                    words, plane = codes[name, n, a]
                    nc.tensor.matmul_mx(
                        out=banks[bank][:, c0 - base:c1 - base],
                        lhsT=vw[a][:, cols].bitcast(FP8X4), lhsT_scale=vs[ROWS * a:P, cols],
                        rhs=words[:].bitcast(FP8X4), rhs_scale=plane[:],
                        start=(a == 0), stop=(a == PASSES - 1),
                    )
            width = PIECES[name][ns[-1]][1] - base
            g, first = divmod(base, KP)
            sums[name, ns[0], c] = (
                banks[bank][:, 0:width].rearrange("p (m t) -> p t m", t=PACK), g,
                slice(first // PACK, (first + width) // PACK),
            )

        turns = {}

        def count_turns(n, c, host=None):
            x, g, ms = sums["w2", n, c]
            if host is None:
                turns[n, c] = ring.tile([P, PACK, ms.stop - ms.start], I32, name="turns", bufs=DEPTH)[:]
            else:
                turns[n, c] = quarters(host.bitcast(I32)[:, 0:KP])
            nc.vector.tensor_scalar(turns[n, c], x, 1.0 / TWO_PI, None, ALU.mult)

        def fraction(n, c):
            x, g, ms = sums["w2", n, c]
            nc.vector.scalar_tensor_tensor(frac[g, c][:, :, ms], x, 1.0 / TWO_PI, turns[n, c], ALU.mult, ALU.subtract)

        wave = {}

        def sine(g, c, host):
            wave[g, c] = quarters(host)
            nc.scalar.activation(wave[g, c], frac[g, c][:], ACT.Sin, scale=TWO_PI)

        form = {}

        def tanh(g, c, host=None):
            x = sums["w1", g, c][0]
            form[g, c] = ring.tile([P, PACK, P], F32, name="form", bufs=DEPTH)[:] if host is None else quarters(host)
            nc.scalar.activation(form[g, c], x, ACT.Tanh)

        look = {}

        def w3_product(g, c, bank):
            look[g, c] = quarters(banks[bank][:])
            cols = slice(c * P, (c + 1) * P)
            v_planes = (vs, vs_low)
            for t in range(PACK):
                c0 = g * KP + t * P
                for a in reversed(range(PASSES)):
                    nc.tensor.matmul_mx(
                        out=look[g, c][:, t, :],
                        lhsT=w3wp[:, a, 2 * c0:2 * (c0 + P)].bitcast(FP4X4), lhsT_scale=w3sp[a][:, c0:c0 + P],
                        rhs=vw[a][:, cols].bitcast(FP8X4), rhs_scale=v_planes[a][:, cols],
                        start=(a == PASSES - 1), stop=(a == 0),
                    )

        both = {}

        def transpose_sum(g, c, bank):
            both[g, c] = quarters(banks[bank][:])
            for t in range(PACK):
                nc.tensor.matmul(both[g, c][:, t, :], form[g, c][:, t, :], ident[:], start=True, stop=False, is_transpose=True)
                nc.tensor.matmul(both[g, c][:, t, :], wave[g, c][:, t, :], ident[:], start=False, stop=True, is_transpose=True)

        gained = {}

        def apply_gain(g, c, host=None):
            gained[g, c] = (
                ring.tile([P, PACK, P], F32, name="gained", bufs=DEPTH)[:] if host is None else quarters(host)
            )
            for t in range(PACK):
                nc.scalar.activation(gained[g, c][:, t, :], both[g, c][:, t, :], ACT.Copy, scale=gain_sb[:, g, t:t + 1])

        hb = {}

        def feature(g, c):
            half, within = divmod(c, 2)
            if within == 0:
                hb[g, half] = ring.tile([P, HALF * PACK], BF16, name="hb", align_bytes=MX_ALIGN)
            nc.vector.tensor_tensor(
                hb[g, half][:, within * KP:(within + 1) * KP].rearrange("p (c x t) -> p c t x", x=RUN, t=PACK),
                look[g, c].rearrange("p t (c x) -> p c t x", x=RUN),
                gained[g, c].rearrange("p t (c x) -> p c t x", x=RUN),
                ALU.max,
            )

        def quantize_h(g, half):
            cols = slice(half * HALF, (half + 1) * HALF)
            nc.vector.quantize_mx(out=hc[g][:, cols].bitcast(FP8X4), scales=hs[g][:, cols], in_=hb[g, half][:])

        energy = {}

        def second_product(m, half, bank):
            rows = slice(m * P, (m + 1) * P)
            cols = slice(half * HALF, (half + 1) * HALF)
            energy[m, half] = banks[bank][:, 0:HALF]
            movers = [(a, vw[a], vs[ROWS * a:P, cols]) for a in range(PASSES)]
            movers = movers + [(g, hc[g], hs[g][:, cols]) for g in range(PASSES)]
            for n, (a, words, plane) in enumerate(movers):
                nc.tensor.matmul_mx(
                    out=energy[m, half],
                    lhsT=v2w[a][:, rows].bitcast(FP8X4), lhsT_scale=v2s[ROWS * a:P, rows],
                    rhs=words[:, cols].bitcast(FP8X4), rhs_scale=plane,
                    start=(n == 0), stop=(n == len(movers) - 1),
                )

        score = {}

        def add_prior(m, half, host=None):
            cols = slice(half * HALF, (half + 1) * HALF)
            if host is None:
                score[m, half] = ring.tile([P, HALF], F32, name="score", bufs=DEPTH)[:]
            else:
                score[m, half] = host.bitcast(F32)[:, 0:HALF]
            nc.vector.tensor_tensor(score[m, half], energy[m, half], prior_sb[m][:, cols], ALU.add)

        def weigh(m):
            nc.scalar.activation(page_weight[m], wgo_sb[:], ACT.Copy, scale=emph_sb[:, m:m + 1])

        def place(m, half):
            cols = slice(half * HALF, (half + 1) * HALF)
            entries = slice(half * HALF // LIST_ROW, (half + 1) * HALF // LIST_ROW)
            nc.vector.tensor_tensor(
                page[m][:].indirect(idx3[:, entries]), score[m, half], page_weight[m][:, cols], ALU.mult
            )

        load_words(tabw, tab_words, 0)
        nc.sync.dma_start(idx[:], offs)
        load_plane(w3s, w3_scales, nc.sync)
        load_words(tabw, tab_words, 1)
        load_plane(tabs, tab_scales, nc.gpsimd)
        load_piece("w2", 0)
        load_piece("w2", 1)
        nc.sync.dma_start(idx2[:], offs2)
        load_piece("w1", 0)
        load_pass("w2", 2, 0)
        nc.sync.dma_start(out=w3w[:].bitcast(I32), in_=w3_words.rearrange("a p c -> p a c").bitcast(I32))
        load_pass("w2", 2, 1)
        load_piece("w1", 1)
        load_piece("w1", 2)
        nc.sync.dma_start(out=gain_sb[:], in_=gain.rearrange("(g p t) -> p g t", g=PASSES, t=PACK))
        for a in range(PASSES):
            load_words(tab2w, tab2_words, a)
        nc.sync.dma_start(idx3[:], offs3)
        with nc.allow_non_contiguous_dma(reason="one emphasis value for each row of the page"):
            nc.sync.dma_start(out=emph_sb[:], in_=emph.rearrange("(m p) -> p m", p=P))
        nc.sync.dma_start(out=wgo_sb[:], in_=wgo)
        for m in range(PAGES):
            nc.sync.dma_start(out=prior_sb[m][:], in_=prior[m * P:(m + 1) * P, :])
            nc.sync.dma_start(out=page[m][:], in_=page1[m * P:(m + 1) * P, :])

        gather_words(vw[0], tabw[0], idx)
        nc.vector.tensor_copy(
            out=w3sp[0][:].rearrange("p (g t m) -> p g t m", g=PASSES, t=PACK),
            in_=w3s[:].rearrange("p (g m t) -> p g t m", g=PASSES, t=PACK),
        )
        lower_plane(w3sp[1], w3sp[0])
        gather_words(vw[1], tabw[1], idx)
        gather_bytes(vs, tabs, idx)
        lower_plane(vs_low, vs)
        load_plane(tab2s, tab2_scales, nc.gpsimd)
        nc.vector.memset(ident[:], 0.0)
        make_identity(nc, ident[:], nomemset=True)

        stream = [("w2", 0), ("w2", 1), ("w1", 0), ("w2", 2), ("w1", 1), ("w1", 2)]
        for step, (name, n) in enumerate(stream):
            for a in range(PASSES):
                quantize_pass(name, n, a, staging[(PASSES * step + a) % STAGING])
        last_stage = staging[(PASSES * len(stream) - 1) % STAGING]

        for n in (0, 1):
            for c in range(BLOCKS):
                product("w2", [n], c, BLOCKS * n + c)
        for n in (0, 1):
            for pair in (FIRST, SECOND):
                for c in pair:
                    count_turns(n, c)
                for c in pair:
                    fraction(n, c)

        for c in FIRST:
            product("w1", [0], c, c)
            sine(0, c, spot("w1", 0, 1, c))
        for a in reversed(range(PASSES)):
            nc.vector.tensor_copy(
                out=w3wp[:, a, :].bitcast(U16).rearrange("p (g t m) -> p g t m", g=PASSES, t=PACK),
                in_=w3w[:, a, :].bitcast(U16).rearrange("p (g m t) -> p g t m", g=PASSES, t=PACK),
            )
        for c in FIRST:
            tanh(0, c, spot("w2", 2, c))
        for c in FIRST:
            product("w2", [2], c, c)
            product("w1", [1, 2], c, 6 + c)
            transpose_sum(0, c, 2 + c)
            w3_product(0, c, 4 + c)
        for c in FIRST:
            count_turns(2, c)
            fraction(2, c)
        for c in FIRST:
            apply_gain(0, c, spot("w1", 1 + c, 1))
        for c in FIRST:
            feature(0, c)
        for c in FIRST:
            sine(1, c, spot("w1", 2, 1 - c, 1 - c))
            tanh(1, c)
        for c in FIRST:
            transpose_sum(1, c, 2 + c)
            w3_product(1, c, 4 + c)
            apply_gain(1, c)
            feature(1, c)
        for g in range(PASSES):
            quantize_h(g, 0)
        gather_bytes(v2s, tab2s, idx2)
        for a in range(PASSES):
            gather_words(v2w[a], tab2w[a], idx2)

        weigh(0)
        for c in SECOND:
            product("w1", [0], c, 4 + c)
        for c in SECOND:
            sine(0, c, spot("w1", c - 1, 1))
            tanh(0, c)
        for m in (0, 1):
            second_product(m, 0, 6 + m)
        for c in SECOND:
            product("w2", [2], c, c - 2)
        for c, host in zip(SECOND, (last_stage, hb[1, 0])):
            count_turns(2, c, host[:])
            fraction(2, c)
        for c in SECOND:
            transpose_sum(0, c, c)
            w3_product(0, c, 2 + c)
            product("w1", [1, 2], c, c - 2)
        weigh(1)
        for c in SECOND:
            apply_gain(0, c)
        for m in (0, 1):
            add_prior(m, 0)
        place(0, 0)
        for m in (2, 3):
            second_product(m, 0, 4 + m)
        weigh(2)
        for c in SECOND:
            sine(1, c, spot("w2", 2, c - 2))
            tanh(1, c)
        weigh(3)
        place(1, 0)
        for c in SECOND:
            feature(0, c)
            transpose_sum(1, c, c)
            w3_product(1, c, 2 + c)
        add_prior(2, 0)
        quantize_h(0, 1)
        for c in SECOND:
            apply_gain(1, c)
        place(2, 0)
        for c in SECOND:
            feature(1, c)
        quantize_h(1, 1)
        add_prior(PAGES - 1, 0, hb[1, 1][:])
        place(PAGES - 1, 0)

        for m, bank in enumerate((6, 7, 0, 1)):
            second_product(m, 1, bank)
        add_prior(0, 1)
        for m in range(PAGES):
            if m + 1 < PAGES:
                add_prior(m + 1, 1)
            place(m, 1)
            nc.sync.dma_start(out=out[m * P:(m + 1) * P, :], in_=page[m][:])
